import numpy as np, ml_dtypes
CORES = [2,6,10,14,18,22,26,30]
N = 8
import mx_ref
BF = ml_dtypes.bfloat16
def gcols(t, e):
    v = np.concatenate([t.reshape(8, 16, -1, 4), np.zeros((8, 16, 1, 4), BF)], axis=2)
    return np.ascontiguousarray(np.stack([v[g][:, e[g]] for g in range(8)])).reshape(128, -1)
def tile(rs):
    return np.stack(rs, axis=2).reshape(128, -1).astype(BF)
def pick(q, e):
    c = np.concatenate([q[0].reshape(128, -1, 4), np.zeros((128, 1, 4), np.uint8)], axis=1); s = np.concatenate([q[1], np.ones((16, 1), np.uint8)], axis=1)
    return (np.ascontiguousarray(c[:, e].reshape(128, -1)), np.ascontiguousarray(s[:, e]))
def join(*qs):
    return (np.concatenate([q[0] for q in qs], axis=1), np.concatenate([q[1] for q in qs], axis=1))
def put(q, e, v):
    c, s = q[0].reshape(128, -1, 4).copy(), q[1].copy(); c[:, e] = v[0].reshape(128, -1, 4); s[:, e] = v[1]
    return (c.reshape(128, -1), s)
def pk(c, s):
    return (np.ascontiguousarray(c), mx_ref.live(s))
def emit(q):
    return q[0], q[1]
def packed(v, rng):
    q = [mx_ref.quantize(np.ascontiguousarray(v[r])) for r in range(N)]
    return np.stack([a for a, b in q]), np.stack([mx_ref.plane(b, rng) for a, b in q])
def f(rng, *shape):
    return mx_ref.flush((rng.standard_normal(shape, dtype=np.float32) * np.exp2(rng.integers(-2, 3, shape[:-1] + (1,)))).astype(BF))
def wide(rng, *shape, cols=0):
    v = rng.standard_normal(shape, dtype=np.float32) * np.exp2(rng.integers(-12, 13, shape)).astype(np.float32)
    if cols: v *= np.repeat(np.exp2(rng.integers(-cols, cols + 1, shape[:-2] + (1, shape[-1] // 4))) * (rng.random(shape[:-2] + (1, shape[-1] // 4)) > 0.0625), 4, axis=-1).astype(np.float32)
    return mx_ref.flush(v.astype(BF))
C, K, R = 512, 128, 4
def lowest(p):
    return np.argsort(p[::16] + np.float32(0.0), axis=1, kind="stable")[:, :K]
def gput(t, e, s):
    o, w = t.reshape(8, 16, -1, 4).copy(), s.reshape(8, 16, -1, 4)
    for g in range(8): o[g][:, e[g]] = w[g]
    return o.reshape(128, -1)
def numbers_of(rng):
    return {"x": np.array(f(rng, N, 128, 4 * C)), "a": np.array(f(rng, N, 128, 4 * K)), "u": np.array(f(rng, N, 128, 512)), "v": np.array(f(rng, N, 128, 512))}
def weights(rng, w):
    c, p = packed(w, rng)
    return {"wc": c, "ws": p}
def still(rng):
    w = np.zeros((N, 128, 4, 128, 4), np.float32)
    i = np.arange(128)
    for b in range(4): w[:, i, b, i, b] = 32
    return weights(rng, w.reshape(N, 128, 2048).astype(BF))
def signs(rng):
    return np.stack([rng.permutation(8) % 2 * 2.0 - 1.0 for r in range(N)])
def digits(rng, t, s):
    x = t.astype(np.float32).reshape(N, 8, 16, -1, 4)
    b = ((s[..., None] >> np.arange(8)) & 1) * np.exp2(np.arange(8) - 23.0)
    x[:, :, 0] = 0
    x[:, :, 0, :, 0] = 1
    x[:, :, 8] = b[..., :4]
    x[:, :, 9] = b[..., 4:]
    z = x[:, :, 10:].shape
    x[:, :, 10:] = rng.integers(4, 8, z) * rng.choice([-1.0, 1.0], z) * 2.0 ** -20
    return x.reshape(t.shape).astype(BF)
def setup_inputs(rng):
    return {**numbers_of(rng), **weights(rng, f(rng, N, 128, 2048))}
def setup_inputs_ties(rng):
    d = numbers_of(rng)
    e = rng.permutation(N)
    for n in ("x", "a"):
        x = d[n].reshape(N, 8, 16, -1, 4)
        for r in range(N):
            k = rng.permutation(x.shape[3]) % 3
            if n == "x" and r == e[0]: k = np.zeros(C, int)
            p = x[r][:, :8, :3].copy()
            p[:, :, 2] = 0
            x[r][:, :8] = p[:, :, k]
        if n == "x": x[e[1]] = 0
        d[n] = x.reshape(N, 128, -1)
    u = d["u"].reshape(N, 8, 16, 128, 4)
    u[:, :, 8:, ::16] = 0
    w = np.array(f(rng, N, 128, 2048)).reshape(N, 8, 16, 4, 8, 16, 4)
    w[:, :, 8:, :, :, :8] = 0
    return {"x": d["x"], "a": d["a"], "u": u.reshape(N, 128, 512), "v": d["v"], **weights(rng, w.reshape(N, 128, 2048))}
def setup_inputs_near(rng):
    d = numbers_of(rng)
    turn = (1.0 - 2.0 * (np.arange(N) % 2))[:, None]
    g = signs(rng)[:1] * turn
    h = rng.choice([-1.0, 1.0], 8)[None, :] * turn
    size = np.where(signs(rng) > 0, 1.0, 2.0 ** -28)
    shift = np.stack([2 + 2 * rng.permutation(C // 2 - K - 1)[:8] for r in range(N)])
    shift[np.arange(N), np.argmax(g, axis=1)] = 0
    q = (C - 1 - np.arange(C) - shift[:, :, None]) % C // 2
    k = K // 2 + (K - np.arange(K)) // 2 + np.zeros((N, 8, 1), int)
    up = h[:, :, None] > 0
    d["x"] = digits(rng, d["x"], np.where(up, q, C // 2 - 1 - q))
    d["a"] = digits(rng, d["a"], np.where(up, k, C // 2 - 1 - k))
    far = np.where(g > 0, np.argmax(q, axis=2), np.argmin(q, axis=2))
    x = d["x"].reshape(N, 8, 16, C, 4)
    x[np.arange(N)[:, None], np.arange(8)[None, :], 0, far, 0] = 4096
    g = (g * size).astype(np.float32).astype(BF)
    h = (h * size).astype(np.float32).astype(BF)
    u = d["u"].reshape(N, 128, 128, 4)
    u[:, :, ::16] = 0
    for i in range(8):
        u[:, 16 * i, 16 * i, 0] = g[:, i]
        u[:, 16 * i + 8:16 * i + 10, 16 * i] = h[:, i, None, None]
    return {"x": x.reshape(N, 128, 4 * C), "a": d["a"], "u": u.reshape(N, 128, 512), "v": d["v"], **still(rng)}
def setup_inputs_huge(rng):
    d = numbers_of(rng)
    both = rng.permutation(N) % 2 == 0
    k = np.stack([rng.permutation(C) % 2 for r in range(N)])
    k[~both] = -1
    x = 2.0 ** 30 * (0.6 + 0.4 * rng.random((N, 8, 16, C, 4)))
    x[:, :, :8] *= np.where(k == 1, 2.0 ** -6, 1.0)[:, None, None, :, None]
    x[:, :, 8:] *= np.where(k == 0, 2.0 ** -6, 1.0)[:, None, None, :, None]
    a = 2.0 ** 30 * (0.6 + 0.4 * rng.random((N, 128, 4 * K)))
    s = np.ones((N, 8, 16, 1, 1))
    s[both, :, 8:] = -1
    s = s * signs(rng)[:, None, None, :, None] * 2.0 ** 30 * (1 - 0.25 * rng.random((N, 8, 16, 8, 4)))
    u = d["u"].reshape(N, 8, 16, 128, 4)
    u[:, :, :, ::16] = s.astype(np.float32).astype(BF)
    return {"x": x.astype(np.float32).reshape(N, 128, 4 * C).astype(BF), "a": a.astype(np.float32).astype(BF), "u": u.reshape(N, 128, 512), "v": d["v"], **still(rng)}
def setup_inputs_spread(rng):
    d = setup_inputs(rng)
    d["x"] = wide(rng, N, 128, 4 * C, cols=6)
    d["a"] = wide(rng, N, 128, 4 * K, cols=6)
    return d
def check_inputs(d):
    b = []
    for k in ("x", "a", "u", "v"):
        z = np.abs(d[k].astype(np.float32))
        if not (np.isfinite(z).all() and ((z == 0) | (z >= 2.0 ** -30) & (z <= 2.0 ** 30)).all()): b.append("a value of " + k)
    top = np.max((d["wc"] & 127).reshape(N, 16, 8, -1, 4), axis=(2, 4))
    s = np.stack([mx_ref.live(p) for p in d["ws"]])
    if (top == 127).any(): b.append("a code of wc")
    if not ((top == 0) & (s == 1) | (top > 0) & (s >= 88) & (s <= 157)).all(): b.append("a scale of ws")
    return b
def reference(x, a, u, v, wc, ws):
    qu = [mx_ref.quantize(u[r]) for r in range(N)]
    lay = [pk(wc[r], ws[r]) for r in range(N)]
    now = [x[r] for r in range(N)]
    came = [mx_ref.quantize(a[r]) for r in range(N)]
    for t in range(R):
        o, gone = [], []
        for r in range(N):
            o.append(lowest(mx_ref.matmul(qu[r], mx_ref.quantize(now[r]))))
            gone.append(mx_ref.quantize(gcols(now[r], o[r])))
            e = tile([np.maximum(mx_ref.matmul(pick(lay[r], np.arange(128 * b, 128 * b + 128)), came[r]), np.float32(0.0)) * np.float32(0.03125) for b in range(4)])
            now[r] = gput(now[r], o[r], e)
        came = [gone[(r - 1) % N] for r in range(N)]
    y, ol = np.zeros((N, 128, C), np.float32), np.zeros((N, 8, K), np.float32)
    oc, osc = np.zeros((N, 128, 4 * C), np.uint8), np.zeros((N, 16, C), np.uint8)
    for r in range(N):
        q = mx_ref.quantize(now[r])
        y[r] = mx_ref.matmul(mx_ref.quantize(v[r]), q)
        ol[r] = o[r]
        oc[r], osc[r] = emit(q)
    return {"y": y, "ol": ol, "oc": oc, "osc": osc}

@@ -1,0 +1,382 @@
+from concourse.mybir import dt, AluOpType, ActivationFunctionType
+
+A = AluOpType
+F = ActivationFunctionType
+ROUNDS = 4
+HALF = 256
+K = 128
+NX = 0
+CUT = 12
+SLOT = 272
+SLOT2 = 144
+MERGE = 584
+CODE = "float8_e4m3fn_x4"
+
+
+def _sb(n, d):
+    return ("sbuf", [128, n], d)
+
+
+SCRATCH = {
+    "ut": _sb(512, "bfloat16"), "vt": _sb(512, "bfloat16"), "at": _sb(512, "bfloat16"),
+    "uc": _sb(128, CODE), "us": _sb(128, "uint8"), "uc2": _sb(128, CODE), "us2": _sb(128, "uint8"),
+    "vc": _sb(128, CODE), "vs": _sb(128, "uint8"),
+    "wcb": _sb(512, CODE), "wsb": _sb(512, "uint8"),
+    "qc": _sb(512, CODE), "qs": _sb(512, "uint8"),
+    "row": _sb(160, "float32"), "col": _sb(160, "float32"), "i16": _sb(256, "float32"), "cnt": _sb(256, "bfloat16"),
+    "c16": _sb(16, "float32"), "cn": _sb(16, "float32"), "ulist": _sb(8, "uint16"), "selo": _sb(2, "uint16"), "ends": _sb(2, "uint16"),
+    "hot": _sb(256, "float32"), "keep0": _sb(256, "float32"), "keepg": _sb(256, "bfloat16"), "keep2": _sb(MERGE, "bfloat16"),
+    "mm": _sb(8, "float32"), "mdiv": _sb(8, "float32"), "thi": _sb(8, "float32"),
+    "ssb": _sb(512, "float32"), "msk": _sb(512, "float32"), "hold": _sb(512, "float32"),
+    "eqs": _sb(512, "bfloat16"), "gate": _sb(512, "bfloat16"),
+    "flag": _sb(256 * (16 + NX), "bfloat16"), "sums": _sb(128 * (16 + NX), "bfloat16"),
+    "sgn": _sb(SLOT * 16, "bfloat16"), "junk": _sb(SLOT * 16, "bfloat16"),
+    "acc1": _sb(16, "float32"), "acc2": _sb(16, "float32"), "s1": _sb(16, "float32"),
+    "off0": _sb(16, "uint16"), "off1": _sb(16, "uint16"),
+    "idx0": _sb(320, "bfloat16"), "idx1": _sb(320, "bfloat16"), "tt0": _sb(288, "bfloat16"), "tt1": _sb(288, "bfloat16"),
+    "lst0": _sb(16, "uint16"), "lst1": _sb(16, "uint16"),
+    "val": _sb(256, "float32"), "msk2": _sb(256, "float32"), "hold2": _sb(256, "float32"),
+    "pay": _sb(256, "float32"), "pay2": _sb(128, "float32"),
+    "f1": _sb(8, "float32"), "f2": _sb(8, "float32"), "fsel": _sb(8, "uint16"),
+    "flag2": _sb(MERGE, "bfloat16"), "cum": _sb(MERGE, "bfloat16"), "sgn2": _sb(SLOT2 * 8, "bfloat16"), "junk2": _sb(SLOT2 * 8, "bfloat16"),
+    "acc3": _sb(16, "float32"), "r1": _sb(16, "float32"), "off2": _sb(8, "uint16"),
+    "ord": _sb(192, "float32"), "tto": _sb(288, "float32"), "lst": _sb(32, "uint16"),
+    "olb": _sb(128, "float32"), "ysb": _sb(512, "float32"),
+    "pd0": ("psum", [128, 512], "float32"), "pd1": ("psum", [128, 512], "float32"),
+    "pa0": ("psum", [128, 512], "float32"), "pa1": ("psum", [128, 512], "float32"),
+}
+for _b in range(4):
+    SCRATCH["pe%d" % _b] = ("psum", [128, 512], "float32")
+for _t in range(ROUNDS + 1):
+    SCRATCH["xs%d" % _t] = _sb(2048, "bfloat16")
+for _t in range(ROUNDS):
+    SCRATCH["et%d" % _t] = _sb(512, "bfloat16")
+    SCRATCH["lc%d" % _t] = _sb(128, CODE)
+    SCRATCH["ls%d" % _t] = _sb(128, "uint8")
+for _t in range(ROUNDS - 1):
+    SCRATCH["pt%d" % _t] = _sb(512, "bfloat16")
+    SCRATCH["pc%d" % _t] = _sb(128, CODE)
+    SCRATCH["ps%d" % _t] = _sb(128, "uint8")
+
+TAGS = ["ldu", "ldx0", "ldx1", "lda", "ldw", "ldv", "cpx", "io1", "io2", "io3", "io4", "io5", "z1", "z2", "k1", "k2", "k3", "k4", "k5", "k6",
+        "qu", "pu", "qa", "qv", "q0", "q1", "qp", "md0", "md1", "ma0", "ma1", "me", "cp0", "cp1", "m0", "m1", "h0", "h1", "e0", "e1", "g0", "g1",
+        "c0", "cx", "s0", "sx", "o0", "ox", "kk", "sg0", "sa0", "sg1", "sa1", "t0", "t1", "u0", "u1", "sc0", "sc1", "sc2",
+        "tr0", "tr1", "l0", "l1", "n0", "n1", "j0", "j1",
+        "v0", "v1", "y0", "y1", "relu", "fa", "fb", "fc", "c2", "sg2", "sa2", "pg", "cu", "ra", "rd", "sco", "tro", "lo",
+        "gp", "scx", "olm", "sto", "yc0", "yc1", "st0", "st1", "st2", "st3", "sent"]
+SEMAPHORES = TAGS + ["arr%d" % _t for _t in range(1, ROUNDS)]
+
+
+def rank_program(g, core, T, topo):
+    rank = T.rank_of(core)
+    if rank is None:
+        return
+    nxt = T.cores[(rank + 1) % len(T.cores)]
+    prv = T.cores[(rank - 1) % len(T.cores)]
+    Q = {"g": g, "v": g.vector, "a": g.scalar, "p": g.tensor, "s": g.sync}
+    ops = []
+    rnd = [0]
+
+    def R(name, a=None, b=None, step=1):
+        n = T[name].shape[1]
+        a = 0 if a is None else a
+        b = n if b is None else b
+        cols = ((1 << (b - a)) - 1) << a if step == 1 else sum(1 << i for i in range(a, b, step))
+        return (T[name][:, a:b:step] if step != 1 else T[name][:, a:b], name, cols)
+
+    def op(q, tag, fn, reads, writes, inc=1, extra=()):
+        ops.append({"q": q, "grp": (tag, rnd[0]), "fn": fn, "inc": inc, "extra": extra,
+                    "r": [x[1:] for x in reads if isinstance(x, tuple)], "w": [x[1:] for x in writes]})
+
+    def ap(x):
+        return x[0] if isinstance(x, tuple) else x
+
+    def ts(tag, out, in0, s1, op0, s2=None, op1=None):
+        if op1 is None:
+            op("v", tag, lambda: g.vector.tensor_scalar(out[0], in0[0], ap(s1), None, op0), [in0, s1], [out])
+        else:
+            op("v", tag, lambda: g.vector.tensor_scalar(out[0], in0[0], ap(s1), ap(s2), op0, op1), [in0, s1, s2], [out])
+
+    def tt(tag, out, in0, in1, o, lst=None):
+        if lst is None:
+            op("v", tag, lambda: g.vector.tensor_tensor(out[0], in0[0], in1[0], o), [in0, in1], [out])
+        else:
+            op("v", tag, lambda: g.vector.tensor_tensor(out[0], in0[0].indirect(lst[0]), in1[0], o), [in0, in1, lst], [out])
+
+    def scan(tag, out, d0, d1, init, op0, op1):
+        op("v", tag, lambda: g.vector.tensor_tensor_scan(out[0], d0[0], d1[0], ap(init), op0, op1), [d0, d1, init], [out])
+
+    def copy(tag, out, in_):
+        op("v", tag, lambda: g.vector.tensor_copy(out[0], in_[0]), [in_], [out])
+
+    def gather(tag, out, win, lst):
+        op("v", tag, lambda: g.vector.tensor_copy(out[0], win[0].indirect(lst[0])), [win, lst], [out])
+
+    def scatter(tag, win, lst, in_):
+        op("v", tag, lambda: g.vector.tensor_copy(win[0].indirect(lst[0]), in_[0]), [in_, lst], [win])
+
+    def turn(tag, out, in_):
+        op("v", tag, lambda: g.vector.transpose(out[0], in_[0]), [in_], [out])
+
+    def fill(tag, out, c):
+        op("v", tag, lambda: g.vector.memset(out[0], c), [], [out])
+
+    def quant(tag, c, s, in_):
+        op("v", tag, lambda: g.vector.quantize_mx(c[0], s[0], in_[0]), [in_], [c, s])
+
+    def act(tag, out, in_, func, bias=0.0, scale=1.0, acc=None, lst=None):
+        def fn():
+            src = in_[0] if lst is None else in_[0].indirect(lst[0])
+            if func is F.Copy:
+                return g.scalar.activation(out[0], src, func) if scale == 1.0 else g.scalar.activation(out[0], src, func, scale=scale)
+            if acc is None:
+                return g.scalar.activation(out[0], src, func, bias=ap(bias), scale=scale)
+            return g.scalar.activation(out[0], src, func, bias=ap(bias), scale=scale, accum_out=acc[0])
+        op("a", tag, fn, [in_, bias, lst], [out] + ([acc] if acc else []))
+
+    def mx(tag, out, wc_, ws_, xc, xs, extra=()):
+        op("p", tag, lambda: g.tensor.matmul_mx(out[0], wc_[0], ws_[0], xc[0], xs[0], True, True), [wc_, ws_, xc, xs], [out], extra=extra)
+
+    def iota(tag, out, pattern, base):
+        op("g", tag, lambda: g.iota(out[0], pattern, base, 0, allow_small_or_imprecise_dtypes=True), [], [out])
+
+    def dma(q, tag, out, in_, reads, writes):
+        op(q, tag, lambda: Q[q].dma_start(out, in_), reads, writes, inc=16)
+
+    def one(name, c):
+        return R(name, c, c + 1)
+
+    def lo(name, h):
+        return R(name, HALF * h, HALF * h + HALF)
+
+    dma("a", "ldu", T.ut[:], T.u[:], [], [R("ut")])
+    dma("s", "ldx1", T.xs0[:, 1024:2048], T.x[:, 1024:2048], [], [R("xs0", 1024, 2048)])
+    dma("a", "ldx0", T.xs0[:, 0:1024], T.x[:, 0:1024], [], [R("xs0", 0, 1024)])
+
+    iota("io1", R("c16"), [[16, 16]], 0)
+    iota("io2", R("row", 32, 64), [[0, 2], [1, 16]], 0)
+    iota("io3", R("i16"), [[0, 16], [1, 16]], 0)
+    iota("io5", R("row", 0, 16), [[1, 2], [32, 4], [160, 2]], 0)
+    iota("io5", R("row", 16, 32), [[1, 2], [32, 4], [-128, 2]], 144)
+    iota("io5", R("row", 64, 96), [[0, 8], [1, 4]], 0)
+    iota("io5", R("row", 96, 128), [[0, 4], [162, 8]], 16)
+    iota("io5", R("row", 128, 160), [[0, 4], [-146, 8]], 1167)
+    iota("io4", R("cnt"), [[1, 256]], 0)
+    for pad in (R("idx0", 0, 32), R("idx1", 256, 288), R("ord"), R("acc2"), R("acc3")):
+        fill("z1", pad, 0.0)
+    fill("z1", R("keep2"), 1.0)
+    copy("k1", R("ulist"), R("c16", 0, 8))
+    ts("k1", R("cn"), R("c16"), -239.0, A.add)
+    turn("k2", R("col", 32, 64), R("row", 32, 64))
+    fill("z2", R("keep2", 0, MERGE, 146), 0.0)
+    fill("z2", R("keep2", 17, MERGE, 162), 0.0)
+    qcol, tcol = one("col", 32), one("col", 64)
+    ts("k3", R("mm"), R("c16", 0, 8), qcol, A.add)
+    ts("k3", R("flag2", 17, MERGE, 162), R("c16", 0, 4), qcol, A.subtract, 15.0, A.add)
+    ts("k3", R("hot"), R("i16"), qcol, A.is_equal)
+    ts("k3", R("keep0"), R("i16"), 0.0, A.not_equal)
+    ts("k3", R("keepg"), R("i16"), qcol, A.is_gt)
+    ts("k5", R("flag2", 0, MERGE, 146), R("mm", 0, 4), -1.0, A.mult, 127.0, A.add)
+    ts("k5", R("mdiv"), R("mm"), 1.0 / K, A.mult)
+    copy("k5", R("sgn2", 15, SLOT2 * 8, SLOT2), R("mm"))
+    turn("k4", R("col", 0, 32), R("row", 0, 32))
+    turn("k4", R("col", 64, 160), R("row", 64, 160))
+    quant("qu", R("uc"), R("us"), R("ut"))
+    copy("k6", one("selo", 0), one("col", 0))
+    op("v", "pu", lambda: g.vector.tensor_copy(T.uc2[:, 0:128].bitcast(dt.uint32), T.uc[:, 0:128].bitcast(dt.uint32).indirect(T.ulist[:, 0:8])),
+       [R("uc"), R("ulist")], [R("uc2")])
+    op("v", "pu", lambda: g.vector.tensor_copy(T.us2[:, 0:128], T.us[:, 0:128].indirect(T.ulist[:, 0:8])), [R("us"), R("ulist")], [R("us2")])
+    ts("k6", one("selo", 1), one("col", 0), 2.0, A.add)
+    ts("k6", one("ends", 0), one("col", 96), one("col", 128), A.min)
+    ts("k6", one("thi", 0), tcol, 1024.0, A.add)
+
+    def quantise_state(t):
+        for h in (1, 0):
+            quant("q%d" % h, lo("qc", h), lo("qs", h), R("xs%d" % t, 1024 * h, 1024 * h + 1024))
+
+    def count_on_vector(tag, h, c, slot):
+        s = one("hold", HALF * h + 16 * c + 15)
+        n = 16 * c + 16
+        ts(tag, R("flag", 256 * slot, 256 * slot + n), R("pd%d" % h, 0, n), s, A.is_le)
+        if n < HALF:
+            ts(tag, R("flag", 256 * slot + n, 256 * slot + HALF), R("pd%d" % h, n, HALF), s, A.is_lt)
+
+    def add_on_vector(tag, h, c, slot):
+        scan(tag, R("sums", 128 * slot, 128 * slot + 128), R("flag", 256 * slot, 256 * slot + 128), R("flag", 256 * slot + 128, 256 * slot + 256),
+             one("gate", HALF * h + 16 * c + 15), A.add, A.add)
+
+    def to_list(h, start, between=()):
+        steps = [
+            lambda: (turn("tr%d" % h, R("tt%d" % h, 0, 128), R("idx%d" % h, start, start + 128)),
+                     turn("tr%d" % h, R("tt%d" % h, 128, 288), R("idx%d" % h, start - 16, start + 144))),
+            lambda: gather("l%d" % h, R("lst%d" % h), R("tt%d" % h), one("selo", 0)),
+            lambda: tt("n%d" % h, R("msk2", K * h, K * h + K), lo("ssb", h), R("hot", 0, K), A.mult, lst=R("lst%d" % h, 0, 8)),
+            lambda: scan("j%d" % h, R("hold2", K * h, K * h + K), R("keep0", 0, K), R("msk2", K * h, K * h + K), 0.0, A.mult, A.add)]
+        for i, step in enumerate(steps):
+            step()
+            if i < len(between):
+                between[i]()
+
+    eng = topo.engines(core, nxt)
+    rid, pid = topo.addr(nxt)[0], topo.addr(nxt)[1]
+    part = len(eng) // 2
+    mask_c = sum(1 << e for e in eng[:part])
+    mask_s = sum(1 << e for e in eng[part:part + part // 2])
+    arrivals = len(topo.engines(prv, core)) // 2
+    arrivals += arrivals // 2
+
+    for t in range(ROUNDS):
+        rnd[0] = t
+        X, Xn, E = "xs%d" % t, "xs%d" % (t + 1), "et%d" % t
+        quantise_state(t)
+        for h in (1, 0):
+            mx("md%d" % h, R("pd%d" % h, 0, HALF), R("uc2"), R("us2"), lo("qc", h), lo("qs", h))
+            mx("ma%d" % h, R("pa%d" % h, 0, HALF), R("uc2"), R("us2"), lo("qc", h), lo("qs", h))
+        if t == 0:
+            dma("s", "lda", T.at[:], T.a[:], [R("xs0")], [R("at")])
+            dma("s", "ldw", T.wcb[:].bitcast(dt.uint8), T.wc[:], [], [R("wcb")])
+            dma("s", "ldw", T.wsb[:], T.ws[:], [], [R("wsb")])
+            dma("s", "ldv", T.vt[:], T.v[:], [], [R("vt")])
+        dma("s", "cpx", T[Xn][:], T[X][:], [R(X)], [R(Xn)])
+        for h in (1, 0):
+            act("cp%d" % h, lo("ssb", h), R("pa%d" % h, 0, HALF), F.Copy)
+
+        tt("m1", lo("msk", 1), R("pd1", 0, HALF), R("hot"), A.mult)
+        if t > 0:
+            p = t - 1
+            quant("qp", R("pc%d" % p), R("ps%d" % p), R("pt%d" % p))
+            op("g", "sent", lambda p=p: g.remote_dma(T["lc%d" % (p + 1)][:].bitcast(dt.uint8), T["pc%d" % p][:].bitcast(dt.uint8),
+                                                     T.sem["arr%d" % (p + 1)], T.sem.sent, pid, rid, mask_c), [R("pc%d" % p)], [], inc=-part)
+            op("g", "sent", lambda p=p: g.remote_dma(T["ls%d" % (p + 1)][:], T["ps%d" % p][:],
+                                                     T.sem["arr%d" % (p + 1)], T.sem.sent, pid, rid, mask_s), [R("ps%d" % p)], [], inc=-(part // 2))
+        scan("h1", lo("hold", 1), R("keep0"), lo("msk", 1), 0.0, A.mult, A.add)
+        tt("m0", lo("msk", 0), R("pd0", 0, HALF), R("hot"), A.mult)
+        tt("e1", lo("eqs", 1), R("pd1", 0, HALF), lo("hold", 1), A.is_equal)
+        scan("h0", lo("hold", 0), R("keep0"), lo("msk", 0), 0.0, A.mult, A.add)
+        scan("g1", lo("gate", 1), R("keepg"), lo("eqs", 1), 0.0, A.mult, A.subtract)
+        tt("e0", lo("eqs", 0), R("pd0", 0, HALF), lo("hold", 0), A.is_equal)
+        tt("kk", R("sgn", SLOT * NX + 15, SLOT * 16, SLOT), R("gate", HALF + 16 * NX + 15, 2 * HALF, 16), R("cn", NX, 16), A.add)
+        for i, (c0, c1) in enumerate(((NX, CUT), (CUT, 16))):
+            for c in range(c0, c1):
+                act("sg%d" % i, R("sgn", SLOT * c + 16, SLOT * c + SLOT), lo("ssb", 1), F.Sign, bias=one("hold", HALF + 16 * c + 15), scale=-1.0)
+            for c in range(c0, c1):
+                a, b, e = SLOT * c + 15, SLOT * c + 16 * c + 32, SLOT * c + SLOT
+                act("sa%d" % i, R("junk", a, b), R("sgn", a, b), F.Relu, scale=-1.0, acc=one("acc1", c))
+                if b < e:
+                    act("sa%d" % i, R("junk", b, e), R("sgn", b, e), F.Relu, acc=one("acc2", c))
+        scan("g0", lo("gate", 0), R("keepg"), lo("eqs", 0), 0.0, A.mult, A.subtract)
+        for c in range(16):
+            count_on_vector("c0", 0, c, c)
+        for c in range(NX):
+            count_on_vector("cx", 1, c, 16 + c)
+        if t == 0:
+            quant("qa", R("lc0"), R("ls0"), R("at"))
+        for b in range(4):
+            mx("me", R("pe%d" % b, 0, K), R("wcb", K * b, K * b + K), R("wsb", K * b, K * b + K), R("lc%d" % t), R("ls%d" % t),
+               extra=(("arr%d" % t, arrivals),) if t > 0 and b == 0 else ())
+        for c in range(16):
+            add_on_vector("s0", 0, c, c)
+        for c in range(NX):
+            add_on_vector("sx", 1, c, 16 + c)
+        if t == 1:
+            quant("qv", R("vc"), R("vs"), R("vt"))
+        copy("o0", R("off0"), R("sums", 127, 128 * 16, 128))
+        if NX:
+            ts("ox", R("off1", 0, NX), R("sums", 128 * 16 + 127, 128 * (16 + NX), 128), -1.0, A.mult, 255.0, A.add)
+        scatter("sc0", R("idx0", 32, 288), R("off0"), R("cnt"))
+        to_list(0, 32, (lambda: tt("t0", R("s1", NX, CUT), R("acc1", NX, CUT), R("acc2", NX, CUT), A.subtract),
+                        lambda: copy("u0", R("off1", NX, CUT), R("s1", NX, CUT)),
+                        lambda: scatter("sc1", R("idx1", 0, 256), R("off1", 0, CUT), R("cnt", 0, 16 * CUT))))
+        act("y0", R("pay", 0, K), R("idx0", 32, 32 + K), F.Identity, bias=tcol, scale=4.0)
+        act("v0", R("val", 0, K), lo("ssb", 0), F.Copy, lst=R("lst0", 0, 8))
+        for b in range(2):
+            act("relu", R(E, K * b, K * b + K), R("pe%d" % b, 0, K), F.Relu, scale=0.03125)
+        tt("t1", R("s1", CUT, 16), R("acc1", CUT, 16), R("acc2", CUT, 16), A.subtract)
+        copy("u1", R("off1", CUT, 16), R("s1", CUT, 16))
+        scatter("sc2", R("idx1", 0, 256), R("off1", CUT, 16), R("cnt", 16 * CUT, HALF))
+        act("y1", R("pay", K, 2 * K), R("idx1", K, 2 * K), F.Identity, bias=one("thi", 0), scale=4.0)
+        to_list(1, K)
+        act("v1", R("val", K, 2 * K), lo("ssb", 1), F.Copy, lst=R("lst1", 0, 8))
+
+        for c in range(8):
+            act("sg2", R("sgn2", SLOT2 * c + 16, SLOT2 * c + SLOT2 - 16 * c), R("val", K + 16 * c, 2 * K), F.Sign, bias=one("hold2", 16 * c + 15), scale=-1.0)
+        tt("fa", R("f1"), R("hold2", 15, K, 16), R("hold2", K + 15, 2 * K, 16), A.is_gt)
+        for c in range(8):
+            at = 146 * c + 1 if c < 4 else 162 * (7 - c) + 18
+            ts("c2", R("flag2", at, at + 16 * c + 16), R("val", 0, 16 * c + 16), one("hold2", K + 16 * c + 15), A.is_le)
+            if c == 0:
+                tt("fb", R("f2"), R("f1"), R("mdiv"), A.add)
+            if c == 1:
+                ts("fc", R("fsel"), R("f2"), float(K), A.mult)
+        for c in range(8):
+            a, b = SLOT2 * c + 15, SLOT2 * c + SLOT2 - 16 * c
+            act("sa2", R("junk2", a, b), R("sgn2", a, b), F.Relu, acc=one("acc3", c))
+        act("pg", R("pay2"), R("pay"), F.Copy, lst=R("fsel"))
+        for b in range(2, 4):
+            act("relu", R(E, K * b, K * b + K), R("pe%d" % b, 0, K), F.Relu, scale=0.03125)
+        scan("cu", R("cum"), R("keep2"), R("flag2"), 0.0, A.mult, A.add)
+        tt("ra", R("r1"), R("cum"), R("acc3"), A.min, lst=one("ends", 0))
+        copy("rd", R("off2"), R("r1", 0, 8))
+        scatter("sco", R("ord", 32, 32 + K), R("off2"), R("pay2"))
+        turn("tro", R("tto", 0, 128), R("ord", 32, 160))
+        turn("tro", R("tto", 128, 288), R("ord", 16, 176))
+        gather("lo", R("lst"), R("tto"), R("selo", 0, 2))
+        scatter("scx", R(Xn), R("lst"), R(E))
+        if t < ROUNDS - 1:
+            for e in range(4):
+                act("gp", R("pt%d" % t, e, 512, 4), R(X), F.Copy, lst=R("lst", 8 * e, 8 * e + 8))
+        else:
+            act("olm", R("olb"), R("ord", 32, 32 + K), F.Copy, scale=0.25)
+            dma("s", "sto", T.ol[:, :], T.olb[0:128:16, :], [R("olb")], [])
+
+    rnd[0] = ROUNDS
+    quantise_state(ROUNDS)
+    for h in (1, 0):
+        mx("md%d" % h, R("pd%d" % h, 0, HALF), R("vc"), R("vs"), lo("qc", h), lo("qs", h))
+    dma("s", "st0", T.oc[:, 1024:2048], lo("qc", 1)[0].bitcast(dt.uint8), [lo("qc", 1)], [])
+    act("yc1", lo("ysb", 1), R("pd1", 0, HALF), F.Copy)
+    copy("yc0", lo("ysb", 0), R("pd0", 0, HALF))
+    dma("a", "st1", T.y[:, HALF:2 * HALF], T.ysb[:, HALF:2 * HALF], [lo("ysb", 1)], [])
+    dma("s", "st0", T.oc[:, 0:1024], lo("qc", 0)[0].bitcast(dt.uint8), [lo("qc", 0)], [])
+    for k in range(4):
+        dma("s", "st2", T.osc[4 * k:4 * k + 4, :], T.qs[32 * k:32 * k + 4, :], [R("qs")], [])
+    dma("a", "st3", T.y[:, 0:HALF], T.ysb[:, 0:HALF], [lo("ysb", 0)], [])
+
+    total, upto, last = {}, {}, {}
+    for i, o in enumerate(ops):
+        tag = o["grp"][0]
+        total[tag] = total.get(tag, 0) + abs(o["inc"])
+        upto[o["grp"]] = total[tag]
+        last[o["grp"]] = i
+    known = {q: {} for q in Q}
+    clock, seen, touched = {}, {}, {}
+    for i, o in enumerate(ops):
+        q, need = o["q"], []
+        for x, writes in [(x, False) for x in o["r"]] + [(x, True) for x in o["w"]]:
+            for y, wrote, grp in touched.get(x[0], []):
+                if grp != o["grp"] and (writes or wrote) and x[1] & y[1] and grp not in need:
+                    need.append(grp)
+        need.sort(key=lambda grp: -last[grp])
+        for grp in need:
+            if known[q].get(grp[0], 0) >= upto[grp]:
+                continue
+            assert last[grp] < i, (grp, o["grp"])
+            Q[q].wait_ge(T.sem[grp[0]], upto[grp])
+            seen[grp[0]] = max(seen.get(grp[0], 0), upto[grp])
+            for tag, n in clock[grp].items():
+                known[q][tag] = max(known[q].get(tag, 0), n)
+        for name, n in o["extra"]:
+            Q[q].wait_ge(T.sem[name], n)
+        ins = o["fn"]()
+        if o["inc"] > 0:
+            ins.then_inc(T.sem[o["grp"][0]], o["inc"])
+        for x in o["r"]:
+            touched.setdefault(x[0], []).append((x, False, o["grp"]))
+        for x in o["w"]:
+            touched.setdefault(x[0], []).append((x, True, o["grp"]))
+        if last[o["grp"]] == i:
+            clock[o["grp"]] = dict(known[q])
+            clock[o["grp"]][o["grp"][0]] = upto[o["grp"]]
+    for tag in TAGS:
+        if seen.get(tag, 0) < total.get(tag, 0):
+            g.wait_ge(T.sem[tag], total[tag])

@@ -5,8 +5,8 @@ F = ActivationFunctionType
 ROUNDS = 4
 HALF = 256
 K = 128
-NX = 0
-CUT = 12
+CUT = 10
+HEAD = 64
 SLOT = 272
 SLOT2 = 144
 MERGE = 584
@@ -29,7 +29,7 @@ SCRATCH = {
     "mm": _sb(8, "float32"), "mdiv": _sb(8, "float32"), "thi": _sb(8, "float32"),
     "ssb": _sb(512, "float32"), "msk": _sb(512, "float32"), "hold": _sb(512, "float32"),
     "eqs": _sb(512, "bfloat16"), "gate": _sb(512, "bfloat16"),
-    "flag": _sb(256 * (16 + NX), "bfloat16"), "sums": _sb(128 * (16 + NX), "bfloat16"),
+    "flag": _sb(256 * 16, "bfloat16"), "sums": _sb(128 * 16, "bfloat16"),
     "sgn": _sb(SLOT * 16, "bfloat16"), "junk": _sb(SLOT * 16, "bfloat16"),
     "acc1": _sb(16, "float32"), "acc2": _sb(16, "float32"), "s1": _sb(16, "float32"),
     "off0": _sb(16, "uint16"), "off1": _sb(16, "uint16"),
@@ -59,10 +59,10 @@ for _t in range(ROUNDS - 1):
     SCRATCH["ps%d" % _t] = _sb(128, "uint8")
 
 TAGS = ["ldu", "ldx0", "ldx1", "lda", "ldw", "ldv", "cpx", "io1", "io2", "io3", "io4", "io5", "z1", "z2", "k1", "k2", "k3", "k4", "k5", "k6",
-        "qu", "pu", "qa", "qv", "q0", "q1", "qp", "md0", "md1", "ma0", "ma1", "me", "cp0", "cp1", "m0", "m1", "h0", "h1", "e0", "e1", "g0", "g1",
-        "c0", "cx", "s0", "sx", "o0", "ox", "kk", "sg0", "sa0", "sg1", "sa1", "t0", "t1", "u0", "u1", "sc0", "sc1", "sc2",
-        "tr0", "tr1", "l0", "l1", "n0", "n1", "j0", "j1",
-        "v0", "v1", "y0", "y1", "relu", "fa", "fb", "fc", "c2", "sg2", "sa2", "pg", "cu", "ra", "rd", "sco", "tro", "lo",
+        "qu", "pu", "qa", "qv", "q0", "q1", "qp", "md0", "md1", "ma0", "ma1", "me", "cp0", "cp1", "m0", "m1", "m2", "h0", "h1", "h2",
+        "e0", "e1", "g0", "g1", "c0", "c1", "s0", "s1", "o0", "kk", "sg0", "sg1", "sg2", "sg3", "sg4", "sa0", "sa1", "sa2",
+        "t0", "t1", "u0", "u1", "sc0", "sc1", "sc2", "tr0", "tr1", "l0", "l1", "n0", "n1", "j0", "j1",
+        "v0", "v1", "y0", "y1", "relu", "fa", "fb", "fc", "c2", "pg", "cu", "ra", "rd", "sco", "tro", "lo",
         "gp", "scx", "olm", "sto", "yc0", "yc1", "st0", "st1", "st2", "st3", "sent"]
 SEMAPHORES = TAGS + ["arr%d" % _t for _t in range(1, ROUNDS)]
 
@@ -194,28 +194,30 @@ def rank_program(g, core, T, topo):
         for h in (1, 0):
             quant("q%d" % h, lo("qc", h), lo("qs", h), R("xs%d" % t, 1024 * h, 1024 * h + 1024))
 
-    def count_on_vector(tag, h, c, slot):
-        s = one("hold", HALF * h + 16 * c + 15)
-        n = 16 * c + 16
-        ts(tag, R("flag", 256 * slot, 256 * slot + n), R("pd%d" % h, 0, n), s, A.is_le)
-        if n < HALF:
-            ts(tag, R("flag", 256 * slot + n, 256 * slot + HALF), R("pd%d" % h, n, HALF), s, A.is_lt)
+    def own(tag, a, b):
+        h = a // HALF
+        tt(tag, R("msk", a, b), R("pd%d" % h, a - HALF * h, b - HALF * h), R("hot", 0, b - a), A.mult)
 
-    def add_on_vector(tag, h, c, slot):
-        scan(tag, R("sums", 128 * slot, 128 * slot + 128), R("flag", 256 * slot, 256 * slot + 128), R("flag", 256 * slot + 128, 256 * slot + 256),
-             one("gate", HALF * h + 16 * c + 15), A.add, A.add)
+    def keep(tag, a, b):
+        scan(tag, R("hold", a, b), R("keep0", 0, b - a), R("msk", a, b), 0.0, A.mult, A.add)
 
-    def to_list(h, start, between=()):
-        steps = [
-            lambda: (turn("tr%d" % h, R("tt%d" % h, 0, 128), R("idx%d" % h, start, start + 128)),
-                     turn("tr%d" % h, R("tt%d" % h, 128, 288), R("idx%d" % h, start - 16, start + 144))),
-            lambda: gather("l%d" % h, R("lst%d" % h), R("tt%d" % h), one("selo", 0)),
-            lambda: tt("n%d" % h, R("msk2", K * h, K * h + K), lo("ssb", h), R("hot", 0, K), A.mult, lst=R("lst%d" % h, 0, 8)),
-            lambda: scan("j%d" % h, R("hold2", K * h, K * h + K), R("keep0", 0, K), R("msk2", K * h, K * h + K), 0.0, A.mult, A.add)]
-        for i, step in enumerate(steps):
-            step()
-            if i < len(between):
-                between[i]()
+    def signs(tag, c0, c1):
+        for c in range(c0, c1):
+            act(tag, R("sgn", SLOT * c + 16, SLOT * c + SLOT), R("pa1", 0, HALF), F.Sign, bias=one("hold", HALF + 16 * c + 15), scale=-1.0)
+
+    def adds(tag, c0, c1):
+        for c in range(c0, c1):
+            a, b, e = SLOT * c + 15, SLOT * c + 16 * c + 32, SLOT * c + SLOT
+            act(tag, R("junk", a, b), R("sgn", a, b), F.Relu, scale=-1.0, acc=one("acc1", c))
+            if b < e:
+                act(tag, R("junk", b, e), R("sgn", b, e), F.Relu, acc=one("acc2", c))
+
+    def to_list(h, start):
+        return [lambda: (turn("tr%d" % h, R("tt%d" % h, 0, 128), R("idx%d" % h, start, start + 128)),
+                         turn("tr%d" % h, R("tt%d" % h, 128, 288), R("idx%d" % h, start - 16, start + 144))),
+                lambda: gather("l%d" % h, R("lst%d" % h), R("tt%d" % h), one("selo", 0)),
+                lambda: tt("n%d" % h, R("msk2", K * h, K * h + K), lo("ssb", h), R("hot", 0, K), A.mult, lst=R("lst%d" % h, 0, 8)),
+                lambda: scan("j%d" % h, R("hold2", K * h, K * h + K), R("keep0", 0, K), R("msk2", K * h, K * h + K), 0.0, A.mult, A.add)]
 
     eng = topo.engines(core, nxt)
     rid, pid = topo.addr(nxt)[0], topo.addr(nxt)[1]
@@ -237,82 +239,87 @@ def rank_program(g, core, T, topo):
             dma("s", "ldw", T.wcb[:].bitcast(dt.uint8), T.wc[:], [], [R("wcb")])
             dma("s", "ldw", T.wsb[:], T.ws[:], [], [R("wsb")])
             dma("s", "ldv", T.vt[:], T.v[:], [], [R("vt")])
-        dma("s", "cpx", T[Xn][:], T[X][:], [R(X)], [R(Xn)])
-        for h in (1, 0):
-            act("cp%d" % h, lo("ssb", h), R("pa%d" % h, 0, HALF), F.Copy)
-
-        tt("m1", lo("msk", 1), R("pd1", 0, HALF), R("hot"), A.mult)
-        if t > 0:
+        else:
             p = t - 1
             quant("qp", R("pc%d" % p), R("ps%d" % p), R("pt%d" % p))
             op("g", "sent", lambda p=p: g.remote_dma(T["lc%d" % (p + 1)][:].bitcast(dt.uint8), T["pc%d" % p][:].bitcast(dt.uint8),
                                                      T.sem["arr%d" % (p + 1)], T.sem.sent, pid, rid, mask_c), [R("pc%d" % p)], [], inc=-part)
             op("g", "sent", lambda p=p: g.remote_dma(T["ls%d" % (p + 1)][:], T["ps%d" % p][:],
                                                      T.sem["arr%d" % (p + 1)], T.sem.sent, pid, rid, mask_s), [R("ps%d" % p)], [], inc=-(part // 2))
-        scan("h1", lo("hold", 1), R("keep0"), lo("msk", 1), 0.0, A.mult, A.add)
-        tt("m0", lo("msk", 0), R("pd0", 0, HALF), R("hot"), A.mult)
+        dma("s", "cpx", T[Xn][:], T[X][:], [R(X)], [R(Xn)])
+        act("cp1", lo("ssb", 1), R("pa1", 0, HALF), F.Copy)
+
+        own("m2", HALF, HALF + HEAD)
+        own("m1", HALF + HEAD, 2 * HALF)
+        keep("h2", HALF, HALF + HEAD)
+        keep("h1", HALF + HEAD, 2 * HALF)
+        own("m0", 0, HALF)
         tt("e1", lo("eqs", 1), R("pd1", 0, HALF), lo("hold", 1), A.is_equal)
-        scan("h0", lo("hold", 0), R("keep0"), lo("msk", 0), 0.0, A.mult, A.add)
+        keep("h0", 0, HALF)
         scan("g1", lo("gate", 1), R("keepg"), lo("eqs", 1), 0.0, A.mult, A.subtract)
         tt("e0", lo("eqs", 0), R("pd0", 0, HALF), lo("hold", 0), A.is_equal)
-        tt("kk", R("sgn", SLOT * NX + 15, SLOT * 16, SLOT), R("gate", HALF + 16 * NX + 15, 2 * HALF, 16), R("cn", NX, 16), A.add)
-        for i, (c0, c1) in enumerate(((NX, CUT), (CUT, 16))):
-            for c in range(c0, c1):
-                act("sg%d" % i, R("sgn", SLOT * c + 16, SLOT * c + SLOT), lo("ssb", 1), F.Sign, bias=one("hold", HALF + 16 * c + 15), scale=-1.0)
-            for c in range(c0, c1):
-                a, b, e = SLOT * c + 15, SLOT * c + 16 * c + 32, SLOT * c + SLOT
-                act("sa%d" % i, R("junk", a, b), R("sgn", a, b), F.Relu, scale=-1.0, acc=one("acc1", c))
-                if b < e:
-                    act("sa%d" % i, R("junk", b, e), R("sgn", b, e), F.Relu, acc=one("acc2", c))
-        scan("g0", lo("gate", 0), R("keepg"), lo("eqs", 0), 0.0, A.mult, A.subtract)
         for c in range(16):
-            count_on_vector("c0", 0, c, c)
-        for c in range(NX):
-            count_on_vector("cx", 1, c, 16 + c)
+            tag, s, n = "c0" if c < 12 else "c1", one("hold", 16 * c + 15), 16 * c + 16
+            ts(tag, R("flag", 256 * c, 256 * c + n), R("pd0", 0, n), s, A.is_le)
+            if n < HALF:
+                ts(tag, R("flag", 256 * c + n, 256 * c + HALF), R("pd0", n, HALF), s, A.is_lt)
+            if c == 0:
+                tt("kk", R("sgn", 15, SLOT * 16, SLOT), R("gate", HALF + 15, 2 * HALF, 16), R("cn"), A.add)
+                scan("g0", lo("gate", 0), R("keepg"), lo("eqs", 0), 0.0, A.mult, A.subtract)
+        signs("sg0", 0, CUT)
+        signs("sg3", CUT, CUT + 1)
+        adds("sa0", 0, CUT)
+        signs("sg1", CUT + 1, 16)
+        adds("sa1", CUT, 16)
+        act("cp0", lo("ssb", 0), R("pa0", 0, HALF), F.Copy)
         if t == 0:
             quant("qa", R("lc0"), R("ls0"), R("at"))
         for b in range(4):
             mx("me", R("pe%d" % b, 0, K), R("wcb", K * b, K * b + K), R("wsb", K * b, K * b + K), R("lc%d" % t), R("ls%d" % t),
                extra=(("arr%d" % t, arrivals),) if t > 0 and b == 0 else ())
         for c in range(16):
-            add_on_vector("s0", 0, c, c)
-        for c in range(NX):
-            add_on_vector("sx", 1, c, 16 + c)
+            scan("s0" if c < 12 else "s1", R("sums", 128 * c, 128 * c + 128), R("flag", 256 * c, 256 * c + 128), R("flag", 256 * c + 128, 256 * c + 256),
+                 one("gate", 16 * c + 15), A.add, A.add)
         if t == 1:
             quant("qv", R("vc"), R("vs"), R("vt"))
+        la, lb = to_list(0, 32), to_list(1, K)
+        tt("t0", R("s1", 0, CUT), R("acc1", 0, CUT), R("acc2", 0, CUT), A.subtract)
         copy("o0", R("off0"), R("sums", 127, 128 * 16, 128))
-        if NX:
-            ts("ox", R("off1", 0, NX), R("sums", 128 * 16 + 127, 128 * (16 + NX), 128), -1.0, A.mult, 255.0, A.add)
+        copy("u0", R("off1", 0, CUT), R("s1", 0, CUT))
         scatter("sc0", R("idx0", 32, 288), R("off0"), R("cnt"))
-        to_list(0, 32, (lambda: tt("t0", R("s1", NX, CUT), R("acc1", NX, CUT), R("acc2", NX, CUT), A.subtract),
-                        lambda: copy("u0", R("off1", NX, CUT), R("s1", NX, CUT)),
-                        lambda: scatter("sc1", R("idx1", 0, 256), R("off1", 0, CUT), R("cnt", 0, 16 * CUT))))
-        act("y0", R("pay", 0, K), R("idx0", 32, 32 + K), F.Identity, bias=tcol, scale=4.0)
-        act("v0", R("val", 0, K), lo("ssb", 0), F.Copy, lst=R("lst0", 0, 8))
-        for b in range(2):
-            act("relu", R(E, K * b, K * b + K), R("pe%d" % b, 0, K), F.Relu, scale=0.03125)
+        scatter("sc1", R("idx1", 0, 256), R("off1", 0, CUT), R("cnt", 0, 16 * CUT))
+        la[0]()
         tt("t1", R("s1", CUT, 16), R("acc1", CUT, 16), R("acc2", CUT, 16), A.subtract)
+        la[1]()
         copy("u1", R("off1", CUT, 16), R("s1", CUT, 16))
         scatter("sc2", R("idx1", 0, 256), R("off1", CUT, 16), R("cnt", 16 * CUT, HALF))
+        la[2]()
+        lb[0]()
+        la[3]()
+        act("y0", R("pay", 0, K), R("idx0", 32, 32 + K), F.Identity, bias=tcol, scale=4.0)
+        act("v0", R("val", 0, K), lo("ssb", 0), F.Copy, lst=R("lst0", 0, 8))
         act("y1", R("pay", K, 2 * K), R("idx1", K, 2 * K), F.Identity, bias=one("thi", 0), scale=4.0)
-        to_list(1, K)
+        lb[1]()
         act("v1", R("val", K, 2 * K), lo("ssb", 1), F.Copy, lst=R("lst1", 0, 8))
+        lb[2]()
+        lb[3]()
 
         for c in range(8):
-            act("sg2", R("sgn2", SLOT2 * c + 16, SLOT2 * c + SLOT2 - 16 * c), R("val", K + 16 * c, 2 * K), F.Sign, bias=one("hold2", 16 * c + 15), scale=-1.0)
+            act("sg2" if c < 6 else "sg4", R("sgn2", SLOT2 * c + 16, SLOT2 * c + SLOT2 - 16 * c), R("val", K + 16 * c, 2 * K), F.Sign,
+                bias=one("hold2", 16 * c + 15), scale=-1.0)
         tt("fa", R("f1"), R("hold2", 15, K, 16), R("hold2", K + 15, 2 * K, 16), A.is_gt)
         for c in range(8):
             at = 146 * c + 1 if c < 4 else 162 * (7 - c) + 18
             ts("c2", R("flag2", at, at + 16 * c + 16), R("val", 0, 16 * c + 16), one("hold2", K + 16 * c + 15), A.is_le)
-            if c == 0:
+            if c == 3:
                 tt("fb", R("f2"), R("f1"), R("mdiv"), A.add)
-            if c == 1:
+            if c == 6:
                 ts("fc", R("fsel"), R("f2"), float(K), A.mult)
         for c in range(8):
             a, b = SLOT2 * c + 15, SLOT2 * c + SLOT2 - 16 * c
             act("sa2", R("junk2", a, b), R("sgn2", a, b), F.Relu, acc=one("acc3", c))
         act("pg", R("pay2"), R("pay"), F.Copy, lst=R("fsel"))
-        for b in range(2, 4):
+        for b in range(4):
             act("relu", R(E, K * b, K * b + K), R("pe%d" % b, 0, K), F.Relu, scale=0.03125)
         scan("cu", R("cum"), R("keep2"), R("flag2"), 0.0, A.mult, A.add)
         tt("ra", R("r1"), R("cum"), R("acc3"), A.min, lst=one("ends", 0))

@@ -3,14 +3,23 @@ from concourse.mybir import dt, AluOpType, ActivationFunctionType
 A = AluOpType
 F = ActivationFunctionType
 ROUNDS = 4
-HALF = 256
+C = 512
+H = 256
 K = 128
-CUT = 10
+NS = (7, 7)
+NE = 5
 HEAD = 64
-SLOT = 272
-SLOT2 = 144
-MERGE = 584
+MARK = 4
+MID = 128
+TOP = 256
+FREE = 4096.0
+XB = 512
 CODE = "float8_e4m3fn_x4"
+WIDE = (H, H + K)
+RUN = (WIDE[0] + 2, WIDE[1] + 2)
+SLOT = (WIDE[0] + 16, WIDE[1] + 16)
+ORDER = "x00 cpx q1 x01 e0 a04 ma1 g0 a00 cpy s02 x02 md1 kk0 a02 cp1 y02 a01 a03 m0 s01 y01 h0 s00 e1 lda y00 o0 t0 w1 w0 g1 u0 qa kk1 w2 r1 sc0 k6 qp tr1 sent r2 b3 l1 v1 b0 b4 r0 b2 b1 x10 a12 st2 x12 free a14 yc1 a10 a13 a11 x11 y12 y10 y11 s12 me relu s11 s10 t1 o1 ga u1 yc2 gd sc1 ge fr gl trf qv lf mg st3 tro gz lo olm scy q0 scx md0 st4 gp m2 m1 ma0 h2 sto yc0 st1 cp0 st0 h1"
+AHEAD = ("cp0", "h1", "h2", "m1", "m2", "ma0", "md0", "q0", "st0", "st1", "yc0")
 
 
 def _sb(n, d):
@@ -23,34 +32,32 @@ SCRATCH = {
     "vc": _sb(128, CODE), "vs": _sb(128, "uint8"),
     "wcb": _sb(512, CODE), "wsb": _sb(512, "uint8"),
     "qc": _sb(512, CODE), "qs": _sb(512, "uint8"),
-    "row": _sb(160, "float32"), "col": _sb(160, "float32"), "i16": _sb(256, "float32"), "cnt": _sb(256, "bfloat16"),
-    "c16": _sb(16, "float32"), "cn": _sb(16, "float32"), "ulist": _sb(8, "uint16"), "selo": _sb(2, "uint16"), "ends": _sb(2, "uint16"),
-    "hot": _sb(256, "float32"), "keep0": _sb(256, "float32"), "keepg": _sb(256, "bfloat16"), "keep2": _sb(MERGE, "bfloat16"),
-    "mm": _sb(8, "float32"), "mdiv": _sb(8, "float32"), "thi": _sb(8, "float32"),
-    "ssb": _sb(512, "float32"), "msk": _sb(512, "float32"), "hold": _sb(512, "float32"),
-    "eqs": _sb(512, "bfloat16"), "gate": _sb(512, "bfloat16"),
-    "flag": _sb(256 * 16, "bfloat16"), "sums": _sb(128 * 16, "bfloat16"),
-    "sgn": _sb(SLOT * 16, "bfloat16"), "junk": _sb(SLOT * 16, "bfloat16"),
-    "acc1": _sb(16, "float32"), "acc2": _sb(16, "float32"), "s1": _sb(16, "float32"),
-    "off0": _sb(16, "uint16"), "off1": _sb(16, "uint16"),
-    "idx0": _sb(320, "bfloat16"), "idx1": _sb(320, "bfloat16"), "tt0": _sb(288, "bfloat16"), "tt1": _sb(288, "bfloat16"),
-    "lst0": _sb(16, "uint16"), "lst1": _sb(16, "uint16"),
-    "val": _sb(256, "float32"), "msk2": _sb(256, "float32"), "hold2": _sb(256, "float32"),
-    "pay": _sb(256, "float32"), "pay2": _sb(128, "float32"),
-    "f1": _sb(8, "float32"), "f2": _sb(8, "float32"), "fsel": _sb(8, "uint16"),
-    "flag2": _sb(MERGE, "bfloat16"), "cum": _sb(MERGE, "bfloat16"), "sgn2": _sb(SLOT2 * 8, "bfloat16"), "junk2": _sb(SLOT2 * 8, "bfloat16"),
-    "acc3": _sb(16, "float32"), "r1": _sb(16, "float32"), "off2": _sb(8, "uint16"),
-    "ord": _sb(192, "float32"), "tto": _sb(288, "float32"), "lst": _sb(32, "uint16"),
-    "olb": _sb(128, "float32"), "ysb": _sb(512, "float32"),
+    "row": _sb(96, "float32"), "col": _sb(96, "float32"), "i16": _sb(H, "float32"), "cnt": _sb(C, "float32"), "src": _sb(C, "float32"),
+    "c16": _sb(16, "float32"), "cn": _sb(16, "float32"), "ulist": _sb(8, "uint16"), "selo": _sb(2, "uint16"), "selv": _sb(2, "uint16"),
+    "hot": _sb(H, "float32"), "keep0": _sb(H, "float32"), "keepg": _sb(H, "bfloat16"), "ones": _sb(K, "float32"), "pc": _sb(4, "float32"),
+    "blank": _sb(2 * K, "float32"), "rep": _sb(4, "uint16"), "xi": _sb(128, "float32"), "xo": _sb(128, "float32"),
+    "msk": _sb(C, "float32"), "hold": _sb(C, "float32"), "eqs": _sb(C, "bfloat16"), "gate": _sb(C, "bfloat16"),
+    "acc1": _sb(32, "float32"), "acc2": _sb(32, "float32"), "s1": _sb(32, "float32"), "off": _sb(32, "uint16"),
+    "ss0": _sb(H, "float32"), "ss1": _sb(H + 2 * K, "float32"), "ord0": _sb(32 + WIDE[0], "float32"), "ord1": _sb(32 + WIDE[1], "float32"),
+    "tt1": _sb(288, "float32"), "lst1": _sb(16, "uint16"),
+    "fr": _sb(192, "bfloat16"), "ttf": _sb(288, "bfloat16"), "lstf": _sb(16, "uint16"),
+    "top": _sb(192, "float32"), "tto": _sb(288, "float32"), "lst": _sb(32, "uint16"),
+    "ga": _sb(16, "float32"), "gd": _sb(16, "float32"), "ge": _sb(64, "float32"), "gl": _sb(64, "uint16"),
+    "olb": _sb(128, "float32"), "ysb": _sb(C, "float32"),
     "pd0": ("psum", [128, 512], "float32"), "pd1": ("psum", [128, 512], "float32"),
     "pa0": ("psum", [128, 512], "float32"), "pa1": ("psum", [128, 512], "float32"),
 }
+for _r in range(2):
+    SCRATCH["flag%d" % _r] = _sb(RUN[_r] * 16, "bfloat16")
+    SCRATCH["sums%d" % _r] = _sb(RUN[_r] // 2 * 16, "bfloat16")
+    SCRATCH["sgn%d" % _r] = _sb(SLOT[_r] * 16, "bfloat16")
+    SCRATCH["junk%d" % _r] = _sb(SLOT[_r] * 16, "bfloat16")
 for _b in range(4):
     SCRATCH["pe%d" % _b] = ("psum", [128, 512], "float32")
 for _t in range(ROUNDS + 1):
-    SCRATCH["xs%d" % _t] = _sb(2048, "bfloat16")
+    SCRATCH["xs%d" % _t] = _sb(XB + 4 * C, "bfloat16")
+    SCRATCH["xz%d" % _t] = _sb(4 * H, "bfloat16")
 for _t in range(ROUNDS):
-    SCRATCH["et%d" % _t] = _sb(512, "bfloat16")
     SCRATCH["lc%d" % _t] = _sb(128, CODE)
     SCRATCH["ls%d" % _t] = _sb(128, "uint8")
 for _t in range(ROUNDS - 1):
@@ -58,12 +65,14 @@ for _t in range(ROUNDS - 1):
     SCRATCH["pc%d" % _t] = _sb(128, CODE)
     SCRATCH["ps%d" % _t] = _sb(128, "uint8")
 
-TAGS = ["ldu", "ldx0", "ldx1", "lda", "ldw", "ldv", "cpx", "io1", "io2", "io3", "io4", "io5", "z1", "z2", "k1", "k2", "k3", "k4", "k5", "k6",
-        "qu", "pu", "qa", "qv", "q0", "q1", "qp", "md0", "md1", "ma0", "ma1", "me", "cp0", "cp1", "m0", "m1", "m2", "h0", "h1", "h2",
-        "e0", "e1", "g0", "g1", "c0", "c1", "s0", "s1", "o0", "kk", "sg0", "sg1", "sg2", "sg3", "sg4", "sa0", "sa1", "sa2",
-        "t0", "t1", "u0", "u1", "sc0", "sc1", "sc2", "tr0", "tr1", "l0", "l1", "n0", "n1", "j0", "j1",
-        "v0", "v1", "y0", "y1", "relu", "fa", "fb", "fc", "c2", "pg", "cu", "ra", "rd", "sco", "tro", "lo",
-        "gp", "scx", "olm", "sto", "yc0", "yc1", "st0", "st1", "st2", "st3", "sent"]
+TAGS = ["ldu", "ldz", "ldx", "lda", "ldw", "ldv", "io1", "io2", "io3", "io4", "io5", "io6", "z1", "k1", "k2", "k3", "k4", "k5", "k6", "k7",
+        "qu", "pu", "qa", "qv", "q0", "q1", "qp", "md0", "md1", "ma0", "ma1", "me", "m0", "m1", "m2", "h0", "h1", "h2",
+        "tr1", "l1", "v1", "relu", "ga", "gd", "ge", "gl", "gz", "fr", "trf", "lf", "mg", "tro", "lo", "gp", "scx", "scy", "olm", "sto",
+        "yc0", "yc1", "yc2", "st0", "st1", "st2", "st3", "st4", "sent"]
+for _r in range(2):
+    TAGS += [_n + str(_r) for _n in ("e", "g", "cp", "o", "kk", "t", "u", "sc")]
+    TAGS += ["%s%d%d" % (_n, _r, _i) for _n, _m in (("a", 5), ("s", 3), ("x", 3), ("y", 3)) for _i in range(_m)]
+TAGS += ["%s%d" % (_n, _i) for _n, _m in (("b", 5), ("w", 3), ("r", 3), ("cpx", ROUNDS), ("cpy", ROUNDS - 1), ("free", ROUNDS)) for _i in range(_m)]
 SEMAPHORES = TAGS + ["arr%d" % _t for _t in range(1, ROUNDS)]
 
 
@@ -75,7 +84,7 @@ def rank_program(g, core, T, topo):
     prv = T.cores[(rank - 1) % len(T.cores)]
     Q = {"g": g, "v": g.vector, "a": g.scalar, "p": g.tensor, "s": g.sync}
     ops = []
-    rnd = [0]
+    rnd = [-1]
 
     def R(name, a=None, b=None, step=1):
         n = T[name].shape[1]
@@ -84,18 +93,20 @@ def rank_program(g, core, T, topo):
         cols = ((1 << (b - a)) - 1) << a if step == 1 else sum(1 << i for i in range(a, b, step))
         return (T[name][:, a:b:step] if step != 1 else T[name][:, a:b], name, cols)
 
-    def op(q, tag, fn, reads, writes, inc=1, extra=()):
-        ops.append({"q": q, "grp": (tag, rnd[0]), "fn": fn, "inc": inc, "extra": extra,
+    def op(q, tag, fn, reads, writes, inc=1, extra=(), step=None):
+        ops.append({"q": q, "grp": (tag, rnd[0]), "step": step or tag, "fn": fn, "inc": inc, "extra": extra,
                     "r": [x[1:] for x in reads if isinstance(x, tuple)], "w": [x[1:] for x in writes]})
 
     def ap(x):
         return x[0] if isinstance(x, tuple) else x
 
-    def ts(tag, out, in0, s1, op0, s2=None, op1=None):
-        if op1 is None:
-            op("v", tag, lambda: g.vector.tensor_scalar(out[0], in0[0], ap(s1), None, op0), [in0, s1], [out])
-        else:
-            op("v", tag, lambda: g.vector.tensor_scalar(out[0], in0[0], ap(s1), ap(s2), op0, op1), [in0, s1, s2], [out])
+    def ts(tag, out, in0, s1, op0, s2=None, op1=None, lst=None):
+        def fn():
+            src = in0[0] if lst is None else in0[0].indirect(lst[0])
+            if op1 is None:
+                return g.vector.tensor_scalar(out[0], src, ap(s1), None, op0)
+            return g.vector.tensor_scalar(out[0], src, ap(s1), ap(s2), op0, op1)
+        op("v", tag, fn, [in0, s1, s2, lst], [out])
 
     def tt(tag, out, in0, in1, o, lst=None):
         if lst is None:
@@ -115,6 +126,10 @@ def rank_program(g, core, T, topo):
     def scatter(tag, win, lst, in_):
         op("v", tag, lambda: g.vector.tensor_copy(win[0].indirect(lst[0]), in_[0]), [in_, lst], [win])
 
+    def turns(tag, out, name):
+        op("v", tag, lambda: g.vector.transpose(T[out][:, 0:128], T[name][:, 32:160]), [R(name, 32, 160)], [R(out, 0, 128)])
+        op("v", tag, lambda: g.vector.transpose(T[out][:, 128:288], T[name][:, 16:176]), [R(name, 16, 176)], [R(out, 128, 288)])
+
     def turn(tag, out, in_):
         op("v", tag, lambda: g.vector.transpose(out[0], in_[0]), [in_], [out])
 
@@ -130,9 +145,9 @@ def rank_program(g, core, T, topo):
             if func is F.Copy:
                 return g.scalar.activation(out[0], src, func) if scale == 1.0 else g.scalar.activation(out[0], src, func, scale=scale)
             if acc is None:
-                return g.scalar.activation(out[0], src, func, bias=ap(bias), scale=scale)
-            return g.scalar.activation(out[0], src, func, bias=ap(bias), scale=scale, accum_out=acc[0])
-        op("a", tag, fn, [in_, bias, lst], [out] + ([acc] if acc else []))
+                return g.scalar.activation(out[0], src, func, bias=ap(bias), scale=ap(scale))
+            return g.scalar.activation(out[0], src, func, bias=ap(bias), scale=ap(scale), accum_out=acc[0])
+        op("a", tag, fn, [in_, bias, scale, lst], [out] + ([acc] if acc else []))
 
     def mx(tag, out, wc_, ws_, xc, xs, extra=()):
         op("p", tag, lambda: g.tensor.matmul_mx(out[0], wc_[0], ws_[0], xc[0], xs[0], True, True), [wc_, ws_, xc, xs], [out], extra=extra)
@@ -140,84 +155,149 @@ def rank_program(g, core, T, topo):
     def iota(tag, out, pattern, base):
         op("g", tag, lambda: g.iota(out[0], pattern, base, 0, allow_small_or_imprecise_dtypes=True), [], [out])
 
-    def dma(q, tag, out, in_, reads, writes):
-        op(q, tag, lambda: Q[q].dma_start(out, in_), reads, writes, inc=16)
+    def dma(q, tag, out, in_, reads, writes, step=None):
+        op(q, tag, lambda: Q[q].dma_start(out, in_), reads, writes, inc=16, step=step)
+
+    def move(step, t, out, in_):
+        dma("s", step + str(t), out[0], in_[0], [in_], [out], step)
 
     def one(name, c):
         return R(name, c, c + 1)
 
-    def lo(name, h):
-        return R(name, HALF * h, HALF * h + HALF)
+    def lot(name, i, n, m):
+        return name + str(m - 1 if i == n - 1 else i * (m - 1) // (n - 1))
+
+    def base(t, r):
+        return H * ((t + r + 1) % 2)
+
+    def state(t, a, n):
+        return R("xs%d" % t, XB + 4 * a, XB + 4 * (a + n))
+
+    def half(name, t, r):
+        return R(name, base(t, r), base(t, r) + H)
 
     dma("a", "ldu", T.ut[:], T.u[:], [], [R("ut")])
-    dma("s", "ldx1", T.xs0[:, 1024:2048], T.x[:, 1024:2048], [], [R("xs0", 1024, 2048)])
-    dma("a", "ldx0", T.xs0[:, 0:1024], T.x[:, 0:1024], [], [R("xs0", 0, 1024)])
+    dma("s", "ldz", T.xz0[:], T.x[:, 4 * H:4 * C], [], [R("xz0")])
+    dma("a", "ldx", state(0, 0, H)[0], T.x[:, 0:4 * H], [], [state(0, 0, H)])
 
     iota("io1", R("c16"), [[16, 16]], 0)
     iota("io2", R("row", 32, 64), [[0, 2], [1, 16]], 0)
-    iota("io3", R("i16"), [[0, 16], [1, 16]], 0)
+    iota("io3", R("i16"), [[0, H // 16], [1, 16]], 0)
     iota("io5", R("row", 0, 16), [[1, 2], [32, 4], [160, 2]], 0)
     iota("io5", R("row", 16, 32), [[1, 2], [32, 4], [-128, 2]], 144)
     iota("io5", R("row", 64, 96), [[0, 8], [1, 4]], 0)
-    iota("io5", R("row", 96, 128), [[0, 4], [162, 8]], 16)
-    iota("io5", R("row", 128, 160), [[0, 4], [-146, 8]], 1167)
-    iota("io4", R("cnt"), [[1, 256]], 0)
-    for pad in (R("idx0", 0, 32), R("idx1", 256, 288), R("ord"), R("acc2"), R("acc3")):
+    iota("io4", R("cnt"), [[4, C]], 0)
+    iota("io6", R("xi"), [[4 * H, 2], [1 - K, 4], [64, 16]], XB - TOP)
+    for pad in (R("ord0", 0, 32), R("fr"), R("top", 0, 32), R("top", 160, 192), R("blank", K, 2 * K)):
         fill("z1", pad, 0.0)
-    fill("z1", R("keep2"), 1.0)
+    fill("z1", R("ones"), 1.0)
+    for r in range(2):
+        fill("z1", R("flag%d" % r, 0, None, RUN[r]), -float(MID))
+        fill("z1", R("flag%d" % r, RUN[r] - 1, None, RUN[r]), 0.0)
     copy("k1", R("ulist"), R("c16", 0, 8))
-    ts("k1", R("cn"), R("c16"), -239.0, A.add)
+    ts("k1", R("cn"), R("c16"), 16.0 - TOP, A.add)
     turn("k2", R("col", 32, 64), R("row", 32, 64))
-    fill("z2", R("keep2", 0, MERGE, 146), 0.0)
-    fill("z2", R("keep2", 17, MERGE, 162), 0.0)
     qcol, tcol = one("col", 32), one("col", 64)
-    ts("k3", R("mm"), R("c16", 0, 8), qcol, A.add)
-    ts("k3", R("flag2", 17, MERGE, 162), R("c16", 0, 4), qcol, A.subtract, 15.0, A.add)
     ts("k3", R("hot"), R("i16"), qcol, A.is_equal)
     ts("k3", R("keep0"), R("i16"), 0.0, A.not_equal)
     ts("k3", R("keepg"), R("i16"), qcol, A.is_gt)
-    ts("k5", R("flag2", 0, MERGE, 146), R("mm", 0, 4), -1.0, A.mult, 127.0, A.add)
-    ts("k5", R("mdiv"), R("mm"), 1.0 / K, A.mult)
-    copy("k5", R("sgn2", 15, SLOT2 * 8, SLOT2), R("mm"))
+    ts("k3", one("pc", 0), qcol, float(MARK), A.not_equal)
+    ts("k3", one("pc", 1), qcol, float(MARK), A.not_equal, FREE, A.mult)
+    ts("k3", one("pc", 3), qcol, 4.0, A.mult)
     turn("k4", R("col", 0, 32), R("row", 0, 32))
-    turn("k4", R("col", 64, 160), R("row", 64, 160))
+    turn("k4", R("col", 64, 96), R("row", 64, 96))
     quant("qu", R("uc"), R("us"), R("ut"))
-    copy("k6", one("selo", 0), one("col", 0))
+    ts("k5", one("pc", 2), qcol, float(MARK), A.is_equal, tcol, A.add)
     op("v", "pu", lambda: g.vector.tensor_copy(T.uc2[:, 0:128].bitcast(dt.uint32), T.uc[:, 0:128].bitcast(dt.uint32).indirect(T.ulist[:, 0:8])),
        [R("uc"), R("ulist")], [R("uc2")])
     op("v", "pu", lambda: g.vector.tensor_copy(T.us2[:, 0:128], T.us[:, 0:128].indirect(T.ulist[:, 0:8])), [R("us"), R("ulist")], [R("us2")])
-    ts("k6", one("selo", 1), one("col", 0), 2.0, A.add)
-    ts("k6", one("ends", 0), one("col", 96), one("col", 128), A.min)
-    ts("k6", one("thi", 0), tcol, 1024.0, A.add)
+    act("k7", R("src"), R("cnt"), F.Identity, bias=one("pc", 2), scale=one("pc", 0))
+    act("k7", R("blank", 0, K), R("ones"), F.Identity, scale=one("pc", 1))
+    act("k7", R("xo"), R("xi"), F.Identity, bias=one("pc", 3))
 
-    def quantise_state(t):
-        for h in (1, 0):
-            quant("q%d" % h, lo("qc", h), lo("qs", h), R("xs%d" % t, 1024 * h, 1024 * h + 1024))
+    def quantise(t, r):
+        quant("q%d" % r, half("qc", t, r), half("qs", t, r), state(t, base(t, 1), H) if r else R("xz%d" % t))
 
-    def own(tag, a, b):
-        h = a // HALF
-        tt(tag, R("msk", a, b), R("pd%d" % h, a - HALF * h, b - HALF * h), R("hot", 0, b - a), A.mult)
+    def scores(t, r):
+        mx("md%d" % r, R("pd%d" % r, 0, H), R("uc2"), R("us2"), half("qc", t, r), half("qs", t, r))
+        mx("ma%d" % r, R("pa%d" % r, 0, H), R("uc2"), R("us2"), half("qc", t, r), half("qs", t, r))
 
-    def keep(tag, a, b):
-        scan(tag, R("hold", a, b), R("keep0", 0, b - a), R("msk", a, b), 0.0, A.mult, A.add)
+    def own(tag, r, a, b):
+        tt(tag, R("msk", H * r + a, H * r + b), R("pd%d" % r, a, b), R("hot", 0, b - a), A.mult)
 
-    def signs(tag, c0, c1):
-        for c in range(c0, c1):
-            act(tag, R("sgn", SLOT * c + 16, SLOT * c + SLOT), R("pa1", 0, HALF), F.Sign, bias=one("hold", HALF + 16 * c + 15), scale=-1.0)
+    def keep(tag, r, a, b):
+        scan(tag, R("hold", H * r + a, H * r + b), R("keep0", 0, b - a), R("msk", H * r + a, H * r + b), 0.0, A.mult, A.add)
 
-    def adds(tag, c0, c1):
-        for c in range(c0, c1):
-            a, b, e = SLOT * c + 15, SLOT * c + 16 * c + 32, SLOT * c + SLOT
-            act(tag, R("junk", a, b), R("sgn", a, b), F.Relu, scale=-1.0, acc=one("acc1", c))
-            if b < e:
-                act(tag, R("junk", b, e), R("sgn", b, e), F.Relu, acc=one("acc2", c))
+    def count(t, r):
+        w = WIDE[r]
+        lead = K if r and t % 2 else 0
+        s0 = K - lead if r else 0
+        if r and not lead:
+            sc, vc = range(16 - NS[r], 16), range(16 - NS[r])
+            se = sc[NS[r] - NE:]
+        else:
+            sc, vc = range(NS[r]), range(NS[r], 16)
+            se = sc[:NE * r]
+        ss, fl, sg, jk, sm = ["%s%d" % (x, r) for x in ("ss", "flag", "sgn", "junk", "sums")]
+        first = 1 if lead else 0
 
-    def to_list(h, start):
-        return [lambda: (turn("tr%d" % h, R("tt%d" % h, 0, 128), R("idx%d" % h, start, start + 128)),
-                         turn("tr%d" % h, R("tt%d" % h, 128, 288), R("idx%d" % h, start - 16, start + 144))),
-                lambda: gather("l%d" % h, R("lst%d" % h), R("tt%d" % h), one("selo", 0)),
-                lambda: tt("n%d" % h, R("msk2", K * h, K * h + K), lo("ssb", h), R("hot", 0, K), A.mult, lst=R("lst%d" % h, 0, 8)),
-                lambda: scan("j%d" % h, R("hold2", K * h, K * h + K), R("keep0", 0, K), R("msk2", K * h, K * h + K), 0.0, A.mult, A.add)]
+        def mine(name, c):
+            return one(name, H * r + 16 * c + 15)
+
+        def row(a, b, bank):
+            if a >= lead and b <= lead + H and bank:
+                return R(bank + str(r), a - lead, b - lead)
+            return R(ss, s0 + a, s0 + b)
+
+        def sign(tag, c, a, b):
+            s = SLOT[r] * c + 16
+            act(tag, R(sg, s + a, s + b), row(a, b, "" if r else "pa"), F.Sign, bias=mine("hold", c), scale=-1.0)
+
+        def add(tag, c, side):
+            s, cut = SLOT[r] * c + 16, lead + 16 * c + 16
+            if side == 0:
+                act(tag, R(jk, s - 1, s + cut), R(sg, s - 1, s + cut), F.Relu, scale=-1.0, acc=one("acc1", 16 * r + c))
+            else:
+                act(tag, R(jk, s + cut, s + w), R(sg, s + cut, s + w), F.Relu, acc=one("acc2", 16 * r + c))
+
+        def flags(tag, c, side):
+            f, cut = RUN[r] * c + 1, lead + 16 * c + 16
+            a, b, o = (0, cut, A.is_le) if side == 0 else (cut, w, A.is_lt)
+            if a < b:
+                ts(tag, R(fl, f + a, f + b), row(a, b, "pd"), mine("hold", c), o)
+
+        tt("e%d" % r, R("eqs", H * r, H * r + H), R("pd%d" % r, 0, H), R("hold", H * r, H * r + H), A.is_equal)
+        scan("g%d" % r, R("gate", H * r, H * r + H), R("keepg"), R("eqs", H * r, H * r + H), 0.0, A.mult, A.subtract)
+        tt("kk%d" % r, R(sg, SLOT[r] * sc[0] + 15, SLOT[r] * (sc[-1] + 1), SLOT[r]),
+           R("gate", H * r + 16 * sc[0] + 15, H * r + 16 * (sc[-1] + 1), 16), R("cn", lead // 16 + sc[0], lead // 16 + sc[-1] + 1), A.add)
+        act("cp%d" % r, R(ss, K * r, K * r + H), R("pa%d" % r, 0, H), F.Copy)
+        if r:
+            for i, c in enumerate(vc):
+                flags("b%d" % (i // 2), c, first)
+            for i, c in enumerate(se):
+                sign(lot("w", i, len(se), 3), c, lead, lead + H)
+            for i, c in enumerate(se):
+                add(lot("r", i, len(se), 3), c, first)
+            act("v1", R(ss, 0, K) if lead else R(ss, K + H, 2 * K + H), R("ss0"), F.Copy, lst=R("lst1", 0, 8))
+        for i, c in enumerate(vc):
+            if not r:
+                flags("a0%d" % (i // 2), c, 0)
+            flags("a%d%d" % (r, i // 2), c, 1 - first)
+        for i, c in enumerate(sc):
+            sign(lot("x%d" % r, i, len(sc), 3), c, *((0, w) if c not in se else (0, lead) if lead else (H, w)))
+        for i, c in enumerate(sc):
+            for side in (0, 1):
+                if not (c in se and side == first):
+                    add(lot("y%d" % r, i, len(sc), 3), c, side)
+        m = RUN[r] // 2
+        for i, c in enumerate(vc):
+            f = RUN[r] * c
+            scan(lot("s%d" % r, i, len(vc), 3), R(sm, m * c, m * c + m), R(fl, f, f + m), R(fl, f + m, f + 2 * m), mine("gate", c), A.add, A.add)
+        a, b = 16 * r + sc[0], 16 * r + sc[-1] + 1
+        tt("t%d" % r, R("s1", a, b), R("acc1", a, b), R("acc2", a, b), A.subtract)
+        ts("o%d" % r, R("s1", 16 * r + vc[0], 16 * r + vc[-1] + 1), R(sm, m * vc[0] + m - 1, m * (vc[-1] + 1), m), -1.0, A.mult, float(TOP - MID), A.add)
+        ts("u%d" % r, R("off", 16 * r, 16 * r + 16), R("s1", 16 * r, 16 * r + 16), -1.0, A.mult, float(TOP), A.add)
+        scatter("sc%d" % r, R("ord%d" % r, 32, 32 + w), R("off", 16 * r, 16 * r + 16), half("src", t, r))
 
     eng = topo.engines(core, nxt)
     rid, pid = topo.addr(nxt)[0], topo.addr(nxt)[1]
@@ -229,16 +309,25 @@ def rank_program(g, core, T, topo):
 
     for t in range(ROUNDS):
         rnd[0] = t
-        X, Xn, E = "xs%d" % t, "xs%d" % (t + 1), "et%d" % t
-        quantise_state(t)
-        for h in (1, 0):
-            mx("md%d" % h, R("pd%d" % h, 0, HALF), R("uc2"), R("us2"), lo("qc", h), lo("qs", h))
-            mx("ma%d" % h, R("pa%d" % h, 0, HALF), R("uc2"), R("us2"), lo("qc", h), lo("qs", h))
+        X, up = "xs%d" % t, t % 2
+        quantise(t, 0)
+        scores(t, 0)
+        own("m2", 0, 0, HEAD)
+        own("m1", 0, HEAD, H)
+        keep("h2", 0, 0, HEAD)
+        keep("h1", 0, HEAD, H)
+        quantise(t, 1)
+        scores(t, 1)
         if t == 0:
-            dma("s", "lda", T.at[:], T.a[:], [R("xs0")], [R("at")])
-            dma("s", "ldw", T.wcb[:].bitcast(dt.uint8), T.wc[:], [], [R("wcb")])
-            dma("s", "ldw", T.wsb[:], T.ws[:], [], [R("wsb")])
-            dma("s", "ldv", T.vt[:], T.v[:], [], [R("vt")])
+            dma("s", "lda", T.at[:], T.a[:], [R("xz0"), state(0, 0, H)], [R("at")])
+            dma("s", "ldw", T.wcb[:].bitcast(dt.uint8), T.wc[:], [], [R("wcb")], "lda")
+            dma("s", "ldw", T.wsb[:], T.ws[:], [], [R("wsb")], "lda")
+            dma("s", "ldv", T.vt[:], T.v[:], [], [R("vt")], "lda")
+            copy("k6", one("selo", 0), one("col", 0))
+            ts("k6", one("selo", 1), one("col", 0), 2.0, A.add)
+            ts("k6", one("selv", 0), one("col", 0), float(MARK), A.add)
+            ts("k6", R("rep"), R("c16", 0, 4), 0.0, A.mult, qcol, A.add)
+            quant("qa", R("lc0"), R("ls0"), R("at"))
         else:
             p = t - 1
             quant("qp", R("pc%d" % p), R("ps%d" % p), R("pt%d" % p))
@@ -246,108 +335,71 @@ def rank_program(g, core, T, topo):
                                                      T.sem["arr%d" % (p + 1)], T.sem.sent, pid, rid, mask_c), [R("pc%d" % p)], [], inc=-part)
             op("g", "sent", lambda p=p: g.remote_dma(T["ls%d" % (p + 1)][:], T["ps%d" % p][:],
                                                      T.sem["arr%d" % (p + 1)], T.sem.sent, pid, rid, mask_s), [R("ps%d" % p)], [], inc=-(part // 2))
-        dma("s", "cpx", T[Xn][:], T[X][:], [R(X)], [R(Xn)])
-        act("cp1", lo("ssb", 1), R("pa1", 0, HALF), F.Copy)
-
-        own("m2", HALF, HALF + HEAD)
-        own("m1", HALF + HEAD, 2 * HALF)
-        keep("h2", HALF, HALF + HEAD)
-        keep("h1", HALF + HEAD, 2 * HALF)
-        own("m0", 0, HALF)
-        tt("e1", lo("eqs", 1), R("pd1", 0, HALF), lo("hold", 1), A.is_equal)
-        keep("h0", 0, HALF)
-        scan("g1", lo("gate", 1), R("keepg"), lo("eqs", 1), 0.0, A.mult, A.subtract)
-        tt("e0", lo("eqs", 0), R("pd0", 0, HALF), lo("hold", 0), A.is_equal)
-        for c in range(16):
-            tag, s, n = "c0" if c < 12 else "c1", one("hold", 16 * c + 15), 16 * c + 16
-            ts(tag, R("flag", 256 * c, 256 * c + n), R("pd0", 0, n), s, A.is_le)
-            if n < HALF:
-                ts(tag, R("flag", 256 * c + n, 256 * c + HALF), R("pd0", n, HALF), s, A.is_lt)
-            if c == 0:
-                tt("kk", R("sgn", 15, SLOT * 16, SLOT), R("gate", HALF + 15, 2 * HALF, 16), R("cn"), A.add)
-                scan("g0", lo("gate", 0), R("keepg"), lo("eqs", 0), 0.0, A.mult, A.subtract)
-        signs("sg0", 0, CUT)
-        signs("sg3", CUT, CUT + 1)
-        adds("sa0", 0, CUT)
-        signs("sg1", CUT + 1, 16)
-        adds("sa1", CUT, 16)
-        act("cp0", lo("ssb", 0), R("pa0", 0, HALF), F.Copy)
-        if t == 0:
-            quant("qa", R("lc0"), R("ls0"), R("at"))
+        if t == 1:
+            quant("qv", R("vc"), R("vs"), R("vt"))
+        move("free", t, R("ord1", 32, 32 + K), R("blank", K * up, K * up + K))
+        move("cpx", t, state(t + 1, base(t, 0), H), R("xz%d" % t))
+        if t < ROUNDS - 1:
+            move("cpy", t, state(t, base(t, 0), H), R("xz%d" % t))
+        count(t, 0)
+        turns("tr1", "tt1", "ord0")
+        ts("l1", R("lst1"), R("tt1"), 0.25, A.mult, -float(base(t, 0)), A.add, lst=one("selo", 0))
+        own("m0", 1, 0, H)
+        keep("h0", 1, 0, H)
+        count(t, 1)
         for b in range(4):
             mx("me", R("pe%d" % b, 0, K), R("wcb", K * b, K * b + K), R("wsb", K * b, K * b + K), R("lc%d" % t), R("ls%d" % t),
                extra=(("arr%d" % t, arrivals),) if t > 0 and b == 0 else ())
-        for c in range(16):
-            scan("s0" if c < 12 else "s1", R("sums", 128 * c, 128 * c + 128), R("flag", 256 * c, 256 * c + 128), R("flag", 256 * c + 128, 256 * c + 256),
-                 one("gate", 16 * c + 15), A.add, A.add)
-        if t == 1:
-            quant("qv", R("vc"), R("vs"), R("vt"))
-        la, lb = to_list(0, 32), to_list(1, K)
-        tt("t0", R("s1", 0, CUT), R("acc1", 0, CUT), R("acc2", 0, CUT), A.subtract)
-        copy("o0", R("off0"), R("sums", 127, 128 * 16, 128))
-        copy("u0", R("off1", 0, CUT), R("s1", 0, CUT))
-        scatter("sc0", R("idx0", 32, 288), R("off0"), R("cnt"))
-        scatter("sc1", R("idx1", 0, 256), R("off1", 0, CUT), R("cnt", 0, 16 * CUT))
-        la[0]()
-        tt("t1", R("s1", CUT, 16), R("acc1", CUT, 16), R("acc2", CUT, 16), A.subtract)
-        la[1]()
-        copy("u1", R("off1", CUT, 16), R("s1", CUT, 16))
-        scatter("sc2", R("idx1", 0, 256), R("off1", CUT, 16), R("cnt", 16 * CUT, HALF))
-        la[2]()
-        lb[0]()
-        la[3]()
-        act("y0", R("pay", 0, K), R("idx0", 32, 32 + K), F.Identity, bias=tcol, scale=4.0)
-        act("v0", R("val", 0, K), lo("ssb", 0), F.Copy, lst=R("lst0", 0, 8))
-        act("y1", R("pay", K, 2 * K), R("idx1", K, 2 * K), F.Identity, bias=one("thi", 0), scale=4.0)
-        lb[1]()
-        act("v1", R("val", K, 2 * K), lo("ssb", 1), F.Copy, lst=R("lst1", 0, 8))
-        lb[2]()
-        lb[3]()
-
-        for c in range(8):
-            act("sg2" if c < 6 else "sg4", R("sgn2", SLOT2 * c + 16, SLOT2 * c + SLOT2 - 16 * c), R("val", K + 16 * c, 2 * K), F.Sign,
-                bias=one("hold2", 16 * c + 15), scale=-1.0)
-        tt("fa", R("f1"), R("hold2", 15, K, 16), R("hold2", K + 15, 2 * K, 16), A.is_gt)
-        for c in range(8):
-            at = 146 * c + 1 if c < 4 else 162 * (7 - c) + 18
-            ts("c2", R("flag2", at, at + 16 * c + 16), R("val", 0, 16 * c + 16), one("hold2", K + 16 * c + 15), A.is_le)
-            if c == 3:
-                tt("fb", R("f2"), R("f1"), R("mdiv"), A.add)
-            if c == 6:
-                ts("fc", R("fsel"), R("f2"), float(K), A.mult)
-        for c in range(8):
-            a, b = SLOT2 * c + 15, SLOT2 * c + SLOT2 - 16 * c
-            act("sa2", R("junk2", a, b), R("sgn2", a, b), F.Relu, acc=one("acc3", c))
-        act("pg", R("pay2"), R("pay"), F.Copy, lst=R("fsel"))
         for b in range(4):
-            act("relu", R(E, K * b, K * b + K), R("pe%d" % b, 0, K), F.Relu, scale=0.03125)
-        scan("cu", R("cum"), R("keep2"), R("flag2"), 0.0, A.mult, A.add)
-        tt("ra", R("r1"), R("cum"), R("acc3"), A.min, lst=one("ends", 0))
-        copy("rd", R("off2"), R("r1", 0, 8))
-        scatter("sco", R("ord", 32, 32 + K), R("off2"), R("pay2"))
-        turn("tro", R("tto", 0, 128), R("ord", 32, 160))
-        turn("tro", R("tto", 128, 288), R("ord", 16, 176))
+            act("relu", R(X, K * b, K * b + K), R("pe%d" % b, 0, K), F.Relu, scale=0.03125)
+        ts("ga", R("ga"), R("s1", 16, 32), float(TOP - K), A.is_le, FREE, A.mult)
+        tt("gd", R("gd"), R("ga"), R("s1", 16, 32), A.subtract)
+        tt("ge", R("ge"), R("gd"), R("xo", 64 * up, 64 * up + 64), A.min, lst=R("rep"))
+        ts("gl", R("gl"), R("ge"), float(TOP), A.add)
+        for e in range(4):
+            act("gz", R("xz%d" % (t + 1), e, 4 * H, 4), R(X, K * e, XB + 4 * (base(t, 1) + H)), F.Copy, lst=R("gl", 16 * e, 16 * e + 16))
+        scan("fr", R("fr", 33, 32 + K), R("ones", 0, K - 1), R("ord1", 32, 31 + K), 0.0, A.add, A.subtract)
+        turns("trf", "ttf", "fr")
+        gather("lf", R("lstf"), R("ttf"), one("selv", 0))
+        tt("mg", R("top", 32, 32 + K), R("ord0", 32, 32 + K), R("ord1", 32, 32 + K), A.max if up else A.min, lst=R("lstf", 0, 8))
+        turns("tro", "tto", "top")
         gather("lo", R("lst"), R("tto"), R("selo", 0, 2))
-        scatter("scx", R(Xn), R("lst"), R(E))
+        scatter("scy", state(t + 1, 0, C), R("lst", 0, 16), R(X, 0, XB // 2))
+        scatter("scx", state(t + 1, 0, C), R("lst", 16, 32), R(X, XB // 2, XB))
         if t < ROUNDS - 1:
             for e in range(4):
-                act("gp", R("pt%d" % t, e, 512, 4), R(X), F.Copy, lst=R("lst", 8 * e, 8 * e + 8))
+                act("gp", R("pt%d" % t, e, 512, 4), state(t, 0, C), F.Copy, lst=R("lst", 8 * e, 8 * e + 8))
         else:
-            act("olm", R("olb"), R("ord", 32, 32 + K), F.Copy, scale=0.25)
+            act("olm", R("olb"), R("top", 32, 32 + K), F.Copy, scale=0.25)
             dma("s", "sto", T.ol[:, :], T.olb[0:128:16, :], [R("olb")], [])
 
-    rnd[0] = ROUNDS
-    quantise_state(ROUNDS)
-    for h in (1, 0):
-        mx("md%d" % h, R("pd%d" % h, 0, HALF), R("vc"), R("vs"), lo("qc", h), lo("qs", h))
-    dma("s", "st0", T.oc[:, 1024:2048], lo("qc", 1)[0].bitcast(dt.uint8), [lo("qc", 1)], [])
-    act("yc1", lo("ysb", 1), R("pd1", 0, HALF), F.Copy)
-    copy("yc0", lo("ysb", 0), R("pd0", 0, HALF))
-    dma("a", "st1", T.y[:, HALF:2 * HALF], T.ysb[:, HALF:2 * HALF], [lo("ysb", 1)], [])
-    dma("s", "st0", T.oc[:, 0:1024], lo("qc", 0)[0].bitcast(dt.uint8), [lo("qc", 0)], [])
+    t = rnd[0] = ROUNDS
+    a, b = base(t, 0), base(t, 1)
+    quantise(t, 0)
+    mx("md0", R("pd0", 0, H), R("vc"), R("vs"), half("qc", t, 0), half("qs", t, 0))
+    dma("s", "st0", T.oc[:, 4 * a:4 * (a + H)], half("qc", t, 0)[0].bitcast(dt.uint8), [half("qc", t, 0)], [])
+    act("yc0", half("ysb", t, 0), R("pd0", 0, H), F.Copy)
+    dma("a", "st1", T.y[:, a:a + H], T.ysb[:, a:a + H], [half("ysb", t, 0)], [])
+    quantise(t, 1)
+    mx("md1", R("pd1", 0, K), R("vc"), R("vs"), R("qc", b, b + K), R("qs", b, b + K))
+    mx("ma1", R("pa1", 0, K), R("vc"), R("vs"), R("qc", b + K, b + H), R("qs", b + K, b + H))
+    dma("s", "st2", T.oc[:, 4 * b:4 * (b + H)], half("qc", t, 1)[0].bitcast(dt.uint8), [half("qc", t, 1)], [])
+    copy("yc1", R("ysb", b, b + K), R("pd1", 0, K))
+    act("yc2", R("ysb", b + K, b + H), R("pa1", 0, K), F.Copy)
+    dma("a", "st3", T.y[:, b:b + H], T.ysb[:, b:b + H], [half("ysb", t, 1)], [])
     for k in range(4):
-        dma("s", "st2", T.osc[4 * k:4 * k + 4, :], T.qs[32 * k:32 * k + 4, :], [R("qs")], [])
-    dma("a", "st3", T.y[:, 0:HALF], T.ysb[:, 0:HALF], [lo("ysb", 0)], [])
+        dma("s", "st4", T.osc[4 * k:4 * k + 4, :], T.qs[32 * k:32 * k + 4, :], [R("qs")], [])
+
+    place = {x: i for i, x in enumerate(ORDER.split())}
+
+    def when(o):
+        if o["grp"][1] < 0:
+            return (-2, 0)
+        if o["grp"] == ("q1", 0):
+            return (-1, place["q0"])
+        return (o["grp"][1] - (o["step"] in AHEAD), place[o["step"]])
+    if place:
+        ops.sort(key=when)
 
     total, upto, last = {}, {}, {}
     for i, o in enumerate(ops):

@@ -6,20 +6,23 @@ ROUNDS = 4
 C = 512
 H = 256
 K = 128
-NS = (7, 7)
+NS = (6, 7)
 NE = 5
+NV = 3
+NX = 1
 HEAD = 64
 MARK = 4
 MID = 128
 TOP = 256
 FREE = 4096.0
+HUGE = 1e29
 XB = 512
 CODE = "float8_e4m3fn_x4"
-WIDE = (H, H + K)
-RUN = (WIDE[0] + 2, WIDE[1] + 2)
+WIDE = (H, H + 16 + K)
+RUN = (WIDE[0] + 2, WIDE[1])
 SLOT = (WIDE[0] + 16, WIDE[1] + 16)
-ORDER = "x00 cpx q1 x01 e0 a04 ma1 g0 a00 cpy s02 x02 md1 kk0 a02 cp1 y02 a01 a03 m0 s01 y01 h0 s00 e1 lda y00 o0 t0 w1 w0 g1 u0 qa kk1 w2 r1 sc0 k6 qp tr1 sent r2 b3 l1 v1 b0 b4 r0 b2 b1 x10 a12 st2 x12 free a14 yc1 a10 a13 a11 x11 y12 y10 y11 s12 me relu s11 s10 t1 o1 ga u1 yc2 gd sc1 ge fr gl trf qv lf mg st3 tro gz lo olm scy q0 scx md0 st4 gp m2 m1 ma0 h2 sto yc0 st1 cp0 st0 h1"
-AHEAD = ("cp0", "h1", "h2", "m1", "m2", "ma0", "md0", "q0", "st0", "st1", "yc0")
+ORDER = "kf q1 lda k7 cp0 h2 z3 q2 h1 qp sent ke e0 io2 a04 ldu io1 g0 a00 x01 ma1 cp1 kk0 md1 x02 x00 y02 a01 a02 skew cpx s00 a03 s02 free z1 y00 z2 s01 y01 kg w1 w2 t0 io3 qa yc1 qv w0 r1 k2 o0 u0 b0 yc2 sc0 r0 b3 tr1 r2 b1 b4 l1 b2 k1 kc v1 k3 c0 a14 ldx a12 a10 k9 x11 s12 x10 kd y11 a13 x12 y10 me a11 s10 s11 st3 qu pv io5 y12 t1 o1 u1 relu k4 ov sc1 ga cpy io4 fr gd trf ge lf io6 gl mg ldz gv0 tro gz gv1 lo pu st5 gv2 scy gp olm q0 k6 scx st2 md0 ma0 yc0 st0 m2 st4 st1 m1 sto"
+AHEAD = ("io1", "io2", "io3", "io4", "io5", "io6", "k1", "k2", "k3", "k4", "k6", "k9", "kc", "kd", "ldu", "ldx", "ldz", "m1", "m2", "ma0", "md0", "pu", "pv", "q0", "qu", "st0", "st1", "yc0", "z1", "z2", "z3")
 
 
 def _sb(n, d):
@@ -36,10 +39,10 @@ SCRATCH = {
     "c16": _sb(16, "float32"), "cn": _sb(16, "float32"), "ulist": _sb(8, "uint16"), "selo": _sb(2, "uint16"), "selv": _sb(2, "uint16"),
     "hot": _sb(H, "float32"), "keep0": _sb(H, "float32"), "keepg": _sb(H, "bfloat16"), "ones": _sb(K, "float32"), "pc": _sb(4, "float32"),
     "blank": _sb(2 * K, "float32"), "rep": _sb(4, "uint16"), "xi": _sb(128, "float32"), "xo": _sb(128, "float32"),
-    "msk": _sb(C, "float32"), "hold": _sb(C, "float32"), "eqs": _sb(C, "bfloat16"), "gate": _sb(C, "bfloat16"),
+    "msk": _sb(H, "float32"), "hold": _sb(H, "float32"), "eqs": _sb(H, "bfloat16"), "gate": _sb(H, "bfloat16"),
     "acc1": _sb(32, "float32"), "acc2": _sb(32, "float32"), "s1": _sb(32, "float32"), "off": _sb(32, "uint16"),
-    "ss0": _sb(H, "float32"), "ss1": _sb(H + 2 * K, "float32"), "ord0": _sb(32 + WIDE[0], "float32"), "ord1": _sb(32 + WIDE[1], "float32"),
-    "tt1": _sb(288, "float32"), "lst1": _sb(16, "uint16"),
+    "ss0": _sb(H, "float32"), "ss1": _sb(H + 16 + 2 * K, "float32"), "sr": _sb(H, "float32"),
+    "ord0": _sb(32 + H, "float32"), "ord1": _sb(32 + H + K, "float32"), "tt1": _sb(288, "float32"), "lst1": _sb(16, "uint16"),
     "fr": _sb(192, "bfloat16"), "ttf": _sb(288, "bfloat16"), "lstf": _sb(16, "uint16"),
     "top": _sb(192, "float32"), "tto": _sb(288, "float32"), "lst": _sb(32, "uint16"),
     "ga": _sb(16, "float32"), "gd": _sb(16, "float32"), "ge": _sb(64, "float32"), "gl": _sb(64, "uint16"),
@@ -65,14 +68,16 @@ for _t in range(ROUNDS - 1):
     SCRATCH["pc%d" % _t] = _sb(128, CODE)
     SCRATCH["ps%d" % _t] = _sb(128, "uint8")
 
-TAGS = ["ldu", "ldz", "ldx", "lda", "ldw", "ldv", "io1", "io2", "io3", "io4", "io5", "io6", "z1", "k1", "k2", "k3", "k4", "k5", "k6", "k7",
-        "qu", "pu", "qa", "qv", "q0", "q1", "qp", "md0", "md1", "ma0", "ma1", "me", "m0", "m1", "m2", "h0", "h1", "h2",
-        "tr1", "l1", "v1", "relu", "ga", "gd", "ge", "gl", "gz", "fr", "trf", "lf", "mg", "tro", "lo", "gp", "scx", "scy", "olm", "sto",
-        "yc0", "yc1", "yc2", "st0", "st1", "st2", "st3", "st4", "sent"]
+TAGS = ["ldu", "ldz", "ldx", "lda", "ldw", "ldv", "io1", "io2", "io3", "io4", "io5", "io6", "z1", "z2", "z3",
+        "k1", "k2", "k3", "k4", "k6", "k7", "k9", "kc", "kd", "ke", "kf", "kg",
+        "qu", "pu", "pv", "qa", "qv", "q0", "q1", "q2", "qp", "md0", "md1", "ma0", "ma1", "me", "m1", "m2", "h1", "h2", "e0", "g0", "kk0", "c0",
+        "tr1", "l1", "v1", "relu", "ov", "ga", "gd", "ge", "gl", "gz", "fr", "trf", "lf", "mg", "tro", "lo", "gp", "scx", "scy", "olm", "sto",
+        "yc0", "yc1", "yc2", "st0", "st1", "st2", "st3", "st4", "st5", "sent"]
 for _r in range(2):
-    TAGS += [_n + str(_r) for _n in ("e", "g", "cp", "o", "kk", "t", "u", "sc")]
+    TAGS += [_n + str(_r) for _n in ("cp", "o", "t", "u", "sc")]
     TAGS += ["%s%d%d" % (_n, _r, _i) for _n, _m in (("a", 5), ("s", 3), ("x", 3), ("y", 3)) for _i in range(_m)]
-TAGS += ["%s%d" % (_n, _i) for _n, _m in (("b", 5), ("w", 3), ("r", 3), ("cpx", ROUNDS), ("cpy", ROUNDS - 1), ("free", ROUNDS)) for _i in range(_m)]
+TAGS += ["%s%d" % (_n, _i) for _n, _m in (("b", 5), ("w", 3), ("r", 3), ("gv", NV), ("cpx", ROUNDS), ("cpy", ROUNDS - 1), ("free", ROUNDS), ("skew", ROUNDS))
+         for _i in range(_m)]
 SEMAPHORES = TAGS + ["arr%d" % _t for _t in range(1, ROUNDS)]
 
 
@@ -84,7 +89,7 @@ def rank_program(g, core, T, topo):
     prv = T.cores[(rank - 1) % len(T.cores)]
     Q = {"g": g, "v": g.vector, "a": g.scalar, "p": g.tensor, "s": g.sync}
     ops = []
-    rnd = [-1]
+    rnd = [0]
 
     def R(name, a=None, b=None, step=1):
         n = T[name].shape[1]
@@ -182,51 +187,57 @@ def rank_program(g, core, T, topo):
 
     iota("io1", R("c16"), [[16, 16]], 0)
     iota("io2", R("row", 32, 64), [[0, 2], [1, 16]], 0)
+    iota("io2", R("row", 64, 96), [[0, 8], [1, 4]], 1)
     iota("io3", R("i16"), [[0, H // 16], [1, 16]], 0)
+    iota("io4", R("cnt"), [[4, C]], 0)
     iota("io5", R("row", 0, 16), [[1, 2], [32, 4], [160, 2]], 0)
     iota("io5", R("row", 16, 32), [[1, 2], [32, 4], [-128, 2]], 144)
-    iota("io5", R("row", 64, 96), [[0, 8], [1, 4]], 0)
-    iota("io4", R("cnt"), [[4, C]], 0)
     iota("io6", R("xi"), [[4 * H, 2], [1 - K, 4], [64, 16]], XB - TOP)
-    for pad in (R("ord0", 0, 32), R("fr"), R("top", 0, 32), R("top", 160, 192), R("blank", K, 2 * K)):
+    for pad in (R("ord0", 0, 32), R("fr"), R("top", 0, 32), R("top", 160, 192)):
         fill("z1", pad, 0.0)
-    fill("z1", R("ones"), 1.0)
-    for r in range(2):
-        fill("z1", R("flag%d" % r, 0, None, RUN[r]), -float(MID))
-        fill("z1", R("flag%d" % r, RUN[r] - 1, None, RUN[r]), 0.0)
     copy("k1", R("ulist"), R("c16", 0, 8))
     ts("k1", R("cn"), R("c16"), 16.0 - TOP, A.add)
-    turn("k2", R("col", 32, 64), R("row", 32, 64))
+    ts("k1", R("sgn1", 15, SLOT[1] * 8, SLOT[1]), R("c16", 0, 8), K + 15.0 - TOP, A.add)
+    ts("k1", R("sgn1", SLOT[1] * 8 + 15, None, SLOT[1]), R("c16", 8, 16), 15.0 - TOP, A.add)
+    turn("k2", R("col", 32, 96), R("row", 32, 96))
+    fill("z2", R("blank", K, 2 * K), 0.0)
+    fill("z2", R("ones"), 1.0)
+    for r in range(2):
+        fill("z3", R("flag%d" % r, 0, None, RUN[r]), -float(MID))
+    fill("z3", R("flag0", RUN[0] - 1, None, RUN[0]), 0.0)
+    fill("z3", R("ss1", K, K + H + 16), HUGE)
     qcol, tcol = one("col", 32), one("col", 64)
     ts("k3", R("hot"), R("i16"), qcol, A.is_equal)
-    ts("k3", R("keep0"), R("i16"), 0.0, A.not_equal)
-    ts("k3", R("keepg"), R("i16"), qcol, A.is_gt)
-    ts("k3", one("pc", 0), qcol, float(MARK), A.not_equal)
-    ts("k3", one("pc", 1), qcol, float(MARK), A.not_equal, FREE, A.mult)
-    ts("k3", one("pc", 3), qcol, 4.0, A.mult)
-    turn("k4", R("col", 0, 32), R("row", 0, 32))
-    turn("k4", R("col", 64, 96), R("row", 64, 96))
+    act("k9", R("keep0"), R("i16"), F.Sign)
     quant("qu", R("uc"), R("us"), R("ut"))
-    ts("k5", one("pc", 2), qcol, float(MARK), A.is_equal, tcol, A.add)
+    ts("kc", one("pc", 0), qcol, float(MARK), A.not_equal)
+    act("pv", R("us2"), R("us"), F.Copy, lst=R("ulist"))
     op("v", "pu", lambda: g.vector.tensor_copy(T.uc2[:, 0:128].bitcast(dt.uint32), T.uc[:, 0:128].bitcast(dt.uint32).indirect(T.ulist[:, 0:8])),
        [R("uc"), R("ulist")], [R("uc2")])
-    op("v", "pu", lambda: g.vector.tensor_copy(T.us2[:, 0:128], T.us[:, 0:128].indirect(T.ulist[:, 0:8])), [R("us"), R("ulist")], [R("us2")])
+    act("kd", one("pc", 1), one("pc", 0), F.Identity, scale=FREE)
+    act("kd", one("pc", 2), one("pc", 0), F.Identity, bias=tcol, scale=-1.0)
+    act("kd", one("pc", 3), qcol, F.Identity, scale=4.0)
     act("k7", R("src"), R("cnt"), F.Identity, bias=one("pc", 2), scale=one("pc", 0))
-    act("k7", R("blank", 0, K), R("ones"), F.Identity, scale=one("pc", 1))
-    act("k7", R("xo"), R("xi"), F.Identity, bias=one("pc", 3))
+    ts("ke", R("keepg"), R("i16"), qcol, A.is_gt)
+    turn("k4", R("col", 0, 32), R("row", 0, 32))
+    ts("k4", R("rep"), R("c16", 0, 4), 0.0, A.mult, qcol, A.add)
+    copy("k6", one("selo", 0), one("col", 0))
+    ts("k6", one("selo", 1), one("col", 0), 2.0, A.add)
+    ts("k6", one("selv", 0), one("col", 0), float(MARK), A.add)
+    act("kf", R("blank", 0, K), R("ones"), F.Identity, scale=one("pc", 1))
+    act("kg", R("xo"), R("xi"), F.Identity, bias=one("pc", 3))
 
     def quantise(t, r):
         quant("q%d" % r, half("qc", t, r), half("qs", t, r), state(t, base(t, 1), H) if r else R("xz%d" % t))
 
-    def scores(t, r):
-        mx("md%d" % r, R("pd%d" % r, 0, H), R("uc2"), R("us2"), half("qc", t, r), half("qs", t, r))
-        mx("ma%d" % r, R("pa%d" % r, 0, H), R("uc2"), R("us2"), half("qc", t, r), half("qs", t, r))
+    def scores(bank, t, r):
+        mx("m%s%d" % (bank, r), R("p%s%d" % (bank, r), 0, H), R("uc2"), R("us2"), half("qc", t, r), half("qs", t, r))
 
-    def own(tag, r, a, b):
-        tt(tag, R("msk", H * r + a, H * r + b), R("pd%d" % r, a, b), R("hot", 0, b - a), A.mult)
+    def own(tag, a, b):
+        tt(tag, R("msk", a, b), R("pd0", a, b), R("hot", 0, b - a), A.mult)
 
-    def keep(tag, r, a, b):
-        scan(tag, R("hold", H * r + a, H * r + b), R("keep0", 0, b - a), R("msk", H * r + a, H * r + b), 0.0, A.mult, A.add)
+    def keep(tag, a, b):
+        scan(tag, R("hold", a, b), R("keep0", 0, b - a), R("msk", a, b), 0.0, A.mult, A.add)
 
     def count(t, r):
         w = WIDE[r]
@@ -239,52 +250,64 @@ def rank_program(g, core, T, topo):
             sc, vc = range(NS[r]), range(NS[r], 16)
             se = sc[:NE * r]
         ss, fl, sg, jk, sm = ["%s%d" % (x, r) for x in ("ss", "flag", "sgn", "junk", "sums")]
+        vx = (vc[len(vc) - NX:] if lead else vc[:NX]) if r else ()
         first = 1 if lead else 0
 
         def mine(name, c):
-            return one(name, H * r + 16 * c + 15)
+            if r:
+                return one(ss, K + 16 * c + 15) if name == "hold" else 0.0
+            return one(name, 16 * c + 15)
 
         def row(a, b, bank):
-            if a >= lead and b <= lead + H and bank:
-                return R(bank + str(r), a - lead, b - lead)
+            if not r:
+                return R(bank + "0", a, b)
             return R(ss, s0 + a, s0 + b)
 
         def sign(tag, c, a, b):
             s = SLOT[r] * c + 16
-            act(tag, R(sg, s + a, s + b), row(a, b, "" if r else "pa"), F.Sign, bias=mine("hold", c), scale=-1.0)
+            act(tag, R(sg, s + a, s + b), row(a, b, "pa"), F.Sign, bias=mine("hold", c), scale=-1.0)
 
         def add(tag, c, side):
-            s, cut = SLOT[r] * c + 16, lead + 16 * c + 16
+            s, cut = SLOT[r] * c + 16, lead + 16 * c + 16 - r
             if side == 0:
                 act(tag, R(jk, s - 1, s + cut), R(sg, s - 1, s + cut), F.Relu, scale=-1.0, acc=one("acc1", 16 * r + c))
             else:
-                act(tag, R(jk, s + cut, s + w), R(sg, s + cut, s + w), F.Relu, acc=one("acc2", 16 * r + c))
+                act(tag, R(jk, s + cut + r, s + w), R(sg, s + cut + r, s + w), F.Relu, acc=one("acc2", 16 * r + c))
 
-        def flags(tag, c, side):
+        def flags(tag, c, side, only=None):
             f, cut = RUN[r] * c + 1, lead + 16 * c + 16
-            a, b, o = (0, cut, A.is_le) if side == 0 else (cut, w, A.is_lt)
+            a, b, o, d = (0, cut - r, A.is_le, 0) if side == 0 else (cut, w, A.is_lt, r)
+            if only is not None:
+                edge = lead if lead else H + 16
+                a, b = (edge, b) if only == side else (a, edge)
             if a < b:
-                ts(tag, R(fl, f + a, f + b), row(a, b, "pd"), mine("hold", c), o)
+                ts(tag, R(fl, f + a - d, f + b - d), row(a, b, "pd"), mine("hold", c), o)
 
-        tt("e%d" % r, R("eqs", H * r, H * r + H), R("pd%d" % r, 0, H), R("hold", H * r, H * r + H), A.is_equal)
-        scan("g%d" % r, R("gate", H * r, H * r + H), R("keepg"), R("eqs", H * r, H * r + H), 0.0, A.mult, A.subtract)
-        tt("kk%d" % r, R(sg, SLOT[r] * sc[0] + 15, SLOT[r] * (sc[-1] + 1), SLOT[r]),
-           R("gate", H * r + 16 * sc[0] + 15, H * r + 16 * (sc[-1] + 1), 16), R("cn", lead // 16 + sc[0], lead // 16 + sc[-1] + 1), A.add)
-        act("cp%d" % r, R(ss, K * r, K * r + H), R("pa%d" % r, 0, H), F.Copy)
+        if r:
+            act("cp1", R("sr"), R("pa1", 0, H), F.Copy)
+            for q in range(16):
+                dma("s", "skew%d" % t, T.ss1[q:128:16, K + 15 - q:K + 15 - q + H], T.sr[q:128:16, :], [R("sr")], [R("ss1", K, K + H + 16)], "skew")
+        else:
+            tt("e0", R("eqs"), R("pd0", 0, H), R("hold"), A.is_equal)
+            scan("g0", R("gate"), R("keepg"), R("eqs"), 0.0, A.mult, A.subtract)
+            tt("kk0", R(sg, 15, SLOT[0] * NS[0], SLOT[0]), R("gate", 15, 16 * NS[0], 16), R("cn", 0, NS[0]), A.add)
+            act("cp0", R(ss), R("pa0", 0, H), F.Copy)
         if r:
             for i, c in enumerate(vc):
                 flags("b%d" % (i // 2), c, first)
+            for c in vx:
+                flags("c0", c, 1 - first, 0)
             for i, c in enumerate(se):
-                sign(lot("w", i, len(se), 3), c, lead, lead + H)
+                sign(lot("w", i, len(se), 3), c, lead, lead + H + 16)
             for i, c in enumerate(se):
                 add(lot("r", i, len(se), 3), c, first)
-            act("v1", R(ss, 0, K) if lead else R(ss, K + H, 2 * K + H), R("ss0"), F.Copy, lst=R("lst1", 0, 8))
+            gather("v1", R(ss, 0, K) if lead else R(ss, K + H + 16, 2 * K + H + 16), R("ss0"), R("lst1", 0, 8))
         for i, c in enumerate(vc):
             if not r:
                 flags("a0%d" % (i // 2), c, 0)
-            flags("a%d%d" % (r, i // 2), c, 1 - first)
+            flags("a%d%d" % (r, i // 2), c, 1 - first, 1 if c in vx else None)
         for i, c in enumerate(sc):
-            sign(lot("x%d" % r, i, len(sc), 3), c, *((0, w) if c not in se else (0, lead) if lead else (H, w)))
+            sign(lot("x%d" % r, i, len(sc), 3), c, *((0, w) if c not in se else (0, lead) if lead else (H + 16, w)))
         for i, c in enumerate(sc):
             for side in (0, 1):
                 if not (c in se and side == first):
@@ -295,9 +318,12 @@ def rank_program(g, core, T, topo):
             scan(lot("s%d" % r, i, len(vc), 3), R(sm, m * c, m * c + m), R(fl, f, f + m), R(fl, f + m, f + 2 * m), mine("gate", c), A.add, A.add)
         a, b = 16 * r + sc[0], 16 * r + sc[-1] + 1
         tt("t%d" % r, R("s1", a, b), R("acc1", a, b), R("acc2", a, b), A.subtract)
-        ts("o%d" % r, R("s1", 16 * r + vc[0], 16 * r + vc[-1] + 1), R(sm, m * vc[0] + m - 1, m * (vc[-1] + 1), m), -1.0, A.mult, float(TOP - MID), A.add)
-        ts("u%d" % r, R("off", 16 * r, 16 * r + 16), R("s1", 16 * r, 16 * r + 16), -1.0, A.mult, float(TOP), A.add)
-        scatter("sc%d" % r, R("ord%d" % r, 32, 32 + w), R("off", 16 * r, 16 * r + 16), half("src", t, r))
+        ends = R(sm, m * vc[0] + m - 1, m * (vc[-1] + 1), m)
+        ts("o%d" % r, R("off", 16 * r + vc[0], 16 * r + vc[-1] + 1), ends, float(MID), A.add)
+        ts("u%d" % r, R("off", a, b), R("s1", a, b), -1.0, A.mult, float(TOP), A.add)
+        if r:
+            ts("ov", R("s1", 16 + vc[0], 16 + vc[-1] + 1), ends, -1.0, A.mult, float(TOP - MID), A.add)
+        scatter("sc%d" % r, R("ord%d" % r, 32, 32 + H + K * r), R("off", 16 * r, 16 * r + 16), half("src", t, r))
 
     eng = topo.engines(core, nxt)
     rid, pid = topo.addr(nxt)[0], topo.addr(nxt)[1]
@@ -311,22 +337,19 @@ def rank_program(g, core, T, topo):
         rnd[0] = t
         X, up = "xs%d" % t, t % 2
         quantise(t, 0)
-        scores(t, 0)
-        own("m2", 0, 0, HEAD)
-        own("m1", 0, HEAD, H)
-        keep("h2", 0, 0, HEAD)
-        keep("h1", 0, HEAD, H)
+        scores("d", t, 0)
+        scores("a", t, 0)
+        own("m2", 0, HEAD)
+        own("m1", HEAD, H)
+        keep("h2", 0, HEAD)
+        keep("h1", HEAD, H)
         quantise(t, 1)
-        scores(t, 1)
+        scores("a", t, 1)
         if t == 0:
             dma("s", "lda", T.at[:], T.a[:], [R("xz0"), state(0, 0, H)], [R("at")])
             dma("s", "ldw", T.wcb[:].bitcast(dt.uint8), T.wc[:], [], [R("wcb")], "lda")
             dma("s", "ldw", T.wsb[:], T.ws[:], [], [R("wsb")], "lda")
             dma("s", "ldv", T.vt[:], T.v[:], [], [R("vt")], "lda")
-            copy("k6", one("selo", 0), one("col", 0))
-            ts("k6", one("selo", 1), one("col", 0), 2.0, A.add)
-            ts("k6", one("selv", 0), one("col", 0), float(MARK), A.add)
-            ts("k6", R("rep"), R("c16", 0, 4), 0.0, A.mult, qcol, A.add)
             quant("qa", R("lc0"), R("ls0"), R("at"))
         else:
             p = t - 1
@@ -344,8 +367,6 @@ def rank_program(g, core, T, topo):
         count(t, 0)
         turns("tr1", "tt1", "ord0")
         ts("l1", R("lst1"), R("tt1"), 0.25, A.mult, -float(base(t, 0)), A.add, lst=one("selo", 0))
-        own("m0", 1, 0, H)
-        keep("h0", 1, 0, H)
         count(t, 1)
         for b in range(4):
             mx("me", R("pe%d" % b, 0, K), R("wcb", K * b, K * b + K), R("wsb", K * b, K * b + K), R("lc%d" % t), R("ls%d" % t),
@@ -356,8 +377,13 @@ def rank_program(g, core, T, topo):
         tt("gd", R("gd"), R("ga"), R("s1", 16, 32), A.subtract)
         tt("ge", R("ge"), R("gd"), R("xo", 64 * up, 64 * up + 64), A.min, lst=R("rep"))
         ts("gl", R("gl"), R("ge"), float(TOP), A.add)
+        end = XB + 4 * (base(t, 1) + H)
+        for i in range(NV):
+            c = 12 - 4 * i
+            gather("gv%d" % i, R("xz%d" % (t + 1), 64 * c + 3, 64 * c + 256, 4), R(X, 3 * K, end), R("gl", 48 + c, 52 + c))
         for e in range(4):
-            act("gz", R("xz%d" % (t + 1), e, 4 * H, 4), R(X, K * e, XB + 4 * (base(t, 1) + H)), F.Copy, lst=R("gl", 16 * e, 16 * e + 16))
+            c = min(16, 64 - 4 * NV - 16 * e)
+            act("gz", R("xz%d" % (t + 1), e, 64 * c, 4), R(X, K * e, end), F.Copy, lst=R("gl", 16 * e, 16 * e + c))
         scan("fr", R("fr", 33, 32 + K), R("ones", 0, K - 1), R("ord1", 32, 31 + K), 0.0, A.add, A.subtract)
         turns("trf", "ttf", "fr")
         gather("lf", R("lstf"), R("ttf"), one("selv", 0))
@@ -380,26 +406,25 @@ def rank_program(g, core, T, topo):
     dma("s", "st0", T.oc[:, 4 * a:4 * (a + H)], half("qc", t, 0)[0].bitcast(dt.uint8), [half("qc", t, 0)], [])
     act("yc0", half("ysb", t, 0), R("pd0", 0, H), F.Copy)
     dma("a", "st1", T.y[:, a:a + H], T.ysb[:, a:a + H], [half("ysb", t, 0)], [])
-    quantise(t, 1)
-    mx("md1", R("pd1", 0, K), R("vc"), R("vs"), R("qc", b, b + K), R("qs", b, b + K))
-    mx("ma1", R("pa1", 0, K), R("vc"), R("vs"), R("qc", b + K, b + H), R("qs", b + K, b + H))
+    quant("q1", R("qc", b, b + K), R("qs", b, b + K), state(t, b, K))
+    quant("q2", R("qc", b + K, b + H), R("qs", b + K, b + H), state(t, b + K, K))
+    mx("ma1", R("pa1", 0, K), R("vc"), R("vs"), R("qc", b, b + K), R("qs", b, b + K))
+    mx("md1", R("pd1", 0, K), R("vc"), R("vs"), R("qc", b + K, b + H), R("qs", b + K, b + H))
     dma("s", "st2", T.oc[:, 4 * b:4 * (b + H)], half("qc", t, 1)[0].bitcast(dt.uint8), [half("qc", t, 1)], [])
-    copy("yc1", R("ysb", b, b + K), R("pd1", 0, K))
-    act("yc2", R("ysb", b + K, b + H), R("pa1", 0, K), F.Copy)
-    dma("a", "st3", T.y[:, b:b + H], T.ysb[:, b:b + H], [half("ysb", t, 1)], [])
+    act("yc2", R("ysb", b, b + K), R("pa1", 0, K), F.Copy)
+    copy("yc1", R("ysb", b + K, b + H), R("pd1", 0, K))
+    dma("a", "st3", T.y[:, b:b + K], T.ysb[:, b:b + K], [R("ysb", b, b + K)], [])
+    dma("a", "st5", T.y[:, b + K:b + H], T.ysb[:, b + K:b + H], [R("ysb", b + K, b + H)], [])
     for k in range(4):
         dma("s", "st4", T.osc[4 * k:4 * k + 4, :], T.qs[32 * k:32 * k + 4, :], [R("qs")], [])
 
     place = {x: i for i, x in enumerate(ORDER.split())}
 
     def when(o):
-        if o["grp"][1] < 0:
-            return (-2, 0)
         if o["grp"] == ("q1", 0):
             return (-1, place["q0"])
         return (o["grp"][1] - (o["step"] in AHEAD), place[o["step"]])
-    if place:
-        ops.sort(key=when)
+    ops.sort(key=when)
 
     total, upto, last = {}, {}, {}
     for i, o in enumerate(ops):

from concourse.mybir import dt, AluOpType, ActivationFunctionType

A = AluOpType
F = ActivationFunctionType
ROUNDS = 4
C = 512
H = 256
K = 128
NS = (6, 7)
NE = 5
NV = 3
NX = 1
HEAD = 64
MARK = 4
MID = 128
TOP = 256
FREE = 4096.0
HUGE = 1e29
XB = 512
CODE = "float8_e4m3fn_x4"
WIDE = (H, H + 16 + K)
RUN = (WIDE[0] + 2, WIDE[1])
SLOT = (WIDE[0] + 16, WIDE[1] + 16)
ORDER = "kf q1 lda k7 cp0 h2 z3 q2 h1 qp sent ke e0 io2 a04 ldu io1 g0 a00 x01 ma1 cp1 kk0 md1 x02 x00 y02 a01 a02 skew cpx s00 a03 s02 free z1 y00 z2 s01 y01 kg w1 w2 t0 io3 qa yc1 qv w0 r1 k2 o0 u0 b0 yc2 sc0 r0 b3 tr1 r2 b1 b4 l1 b2 k1 kc v1 k3 c0 a14 ldx a12 a10 k9 x11 s12 x10 kd y11 a13 x12 y10 me a11 s10 s11 st3 qu pv io5 y12 t1 o1 u1 relu k4 ov sc1 ga cpy io4 fr gd trf ge lf io6 gl mg ldz gv0 tro gz gv1 lo pu st5 gv2 scy gp olm q0 k6 scx st2 md0 ma0 yc0 st0 m2 st4 st1 m1 sto"
AHEAD = ("io1", "io2", "io3", "io4", "io5", "io6", "k1", "k2", "k3", "k4", "k6", "k9", "kc", "kd", "ldu", "ldx", "ldz", "m1", "m2", "ma0", "md0", "pu", "pv", "q0", "qu", "st0", "st1", "yc0", "z1", "z2", "z3")


def _sb(n, d):
    return ("sbuf", [128, n], d)


SCRATCH = {
    "ut": _sb(512, "bfloat16"), "vt": _sb(512, "bfloat16"), "at": _sb(512, "bfloat16"),
    "uc": _sb(128, CODE), "us": _sb(128, "uint8"), "uc2": _sb(128, CODE), "us2": _sb(128, "uint8"),
    "vc": _sb(128, CODE), "vs": _sb(128, "uint8"),
    "wcb": _sb(512, CODE), "wsb": _sb(512, "uint8"),
    "qc": _sb(512, CODE), "qs": _sb(512, "uint8"),
    "row": _sb(96, "float32"), "col": _sb(96, "float32"), "i16": _sb(H, "float32"), "cnt": _sb(C, "float32"), "src": _sb(C, "float32"),
    "c16": _sb(16, "float32"), "cn": _sb(16, "float32"), "ulist": _sb(8, "uint16"), "selo": _sb(2, "uint16"), "selv": _sb(2, "uint16"),
    "hot": _sb(H, "float32"), "keep0": _sb(H, "float32"), "keepg": _sb(H, "bfloat16"), "ones": _sb(K, "float32"), "pc": _sb(4, "float32"),
    "blank": _sb(2 * K, "float32"), "rep": _sb(4, "uint16"), "xi": _sb(128, "float32"), "xo": _sb(128, "float32"),
    "msk": _sb(H, "float32"), "hold": _sb(H, "float32"), "eqs": _sb(H, "bfloat16"), "gate": _sb(H, "bfloat16"),
    "acc1": _sb(32, "float32"), "acc2": _sb(32, "float32"), "s1": _sb(32, "float32"), "off": _sb(32, "uint16"),
    "ss0": _sb(H, "float32"), "ss1": _sb(H + 16 + 2 * K, "float32"), "sr": _sb(H, "float32"),
    "ord0": _sb(32 + H, "float32"), "ord1": _sb(32 + H + K, "float32"), "tt1": _sb(288, "float32"), "lst1": _sb(16, "uint16"),
    "fr": _sb(192, "bfloat16"), "ttf": _sb(288, "bfloat16"), "lstf": _sb(16, "uint16"),
    "top": _sb(192, "float32"), "tto": _sb(288, "float32"), "lst": _sb(32, "uint16"),
    "ga": _sb(16, "float32"), "gd": _sb(16, "float32"), "ge": _sb(64, "float32"), "gl": _sb(64, "uint16"),
    "olb": _sb(128, "float32"), "ysb": _sb(C, "float32"),
    "pd0": ("psum", [128, 512], "float32"), "pd1": ("psum", [128, 512], "float32"),
    "pa0": ("psum", [128, 512], "float32"), "pa1": ("psum", [128, 512], "float32"),
}
for _r in range(2):
    SCRATCH["flag%d" % _r] = _sb(RUN[_r] * 16, "bfloat16")
    SCRATCH["sums%d" % _r] = _sb(RUN[_r] // 2 * 16, "bfloat16")
    SCRATCH["sgn%d" % _r] = _sb(SLOT[_r] * 16, "bfloat16")
    SCRATCH["junk%d" % _r] = _sb(SLOT[_r] * 16, "bfloat16")
for _b in range(4):
    SCRATCH["pe%d" % _b] = ("psum", [128, 512], "float32")
for _t in range(ROUNDS + 1):
    SCRATCH["xs%d" % _t] = _sb(XB + 4 * C, "bfloat16")
    SCRATCH["xz%d" % _t] = _sb(4 * H, "bfloat16")
for _t in range(ROUNDS):
    SCRATCH["lc%d" % _t] = _sb(128, CODE)
    SCRATCH["ls%d" % _t] = _sb(128, "uint8")
for _t in range(ROUNDS - 1):
    SCRATCH["pt%d" % _t] = _sb(512, "bfloat16")
    SCRATCH["pc%d" % _t] = _sb(128, CODE)
    SCRATCH["ps%d" % _t] = _sb(128, "uint8")

TAGS = ["ldu", "ldz", "ldx", "lda", "ldw", "ldv", "io1", "io2", "io3", "io4", "io5", "io6", "z1", "z2", "z3",
        "k1", "k2", "k3", "k4", "k6", "k7", "k9", "kc", "kd", "ke", "kf", "kg",
        "qu", "pu", "pv", "qa", "qv", "q0", "q1", "q2", "qp", "md0", "md1", "ma0", "ma1", "me", "m1", "m2", "h1", "h2", "e0", "g0", "kk0", "c0",
        "tr1", "l1", "v1", "relu", "ov", "ga", "gd", "ge", "gl", "gz", "fr", "trf", "lf", "mg", "tro", "lo", "gp", "scx", "scy", "olm", "sto",
        "yc0", "yc1", "yc2", "st0", "st1", "st2", "st3", "st4", "st5", "sent"]
for _r in range(2):
    TAGS += [_n + str(_r) for _n in ("cp", "o", "t", "u", "sc")]
    TAGS += ["%s%d%d" % (_n, _r, _i) for _n, _m in (("a", 5), ("s", 3), ("x", 3), ("y", 3)) for _i in range(_m)]
TAGS += ["%s%d" % (_n, _i) for _n, _m in (("b", 5), ("w", 3), ("r", 3), ("gv", NV), ("cpx", ROUNDS), ("cpy", ROUNDS - 1), ("free", ROUNDS), ("skew", ROUNDS))
         for _i in range(_m)]
SEMAPHORES = TAGS + ["arr%d" % _t for _t in range(1, ROUNDS)]


def rank_program(g, core, T, topo):
    rank = T.rank_of(core)
    if rank is None:
        return
    nxt = T.cores[(rank + 1) % len(T.cores)]
    prv = T.cores[(rank - 1) % len(T.cores)]
    Q = {"g": g, "v": g.vector, "a": g.scalar, "p": g.tensor, "s": g.sync}
    ops = []
    rnd = [0]

    def R(name, a=None, b=None, step=1):
        n = T[name].shape[1]
        a = 0 if a is None else a
        b = n if b is None else b
        cols = ((1 << (b - a)) - 1) << a if step == 1 else sum(1 << i for i in range(a, b, step))
        return (T[name][:, a:b:step] if step != 1 else T[name][:, a:b], name, cols)

    def op(q, tag, fn, reads, writes, inc=1, extra=(), step=None):
        ops.append({"q": q, "grp": (tag, rnd[0]), "step": step or tag, "fn": fn, "inc": inc, "extra": extra,
                    "r": [x[1:] for x in reads if isinstance(x, tuple)], "w": [x[1:] for x in writes]})

    def ap(x):
        return x[0] if isinstance(x, tuple) else x

    def ts(tag, out, in0, s1, op0, s2=None, op1=None, lst=None):
        def fn():
            src = in0[0] if lst is None else in0[0].indirect(lst[0])
            if op1 is None:
                return g.vector.tensor_scalar(out[0], src, ap(s1), None, op0)
            return g.vector.tensor_scalar(out[0], src, ap(s1), ap(s2), op0, op1)
        op("v", tag, fn, [in0, s1, s2, lst], [out])

    def tt(tag, out, in0, in1, o, lst=None):
        if lst is None:
            op("v", tag, lambda: g.vector.tensor_tensor(out[0], in0[0], in1[0], o), [in0, in1], [out])
        else:
            op("v", tag, lambda: g.vector.tensor_tensor(out[0], in0[0].indirect(lst[0]), in1[0], o), [in0, in1, lst], [out])

    def scan(tag, out, d0, d1, init, op0, op1):
        op("v", tag, lambda: g.vector.tensor_tensor_scan(out[0], d0[0], d1[0], ap(init), op0, op1), [d0, d1, init], [out])

    def copy(tag, out, in_):
        op("v", tag, lambda: g.vector.tensor_copy(out[0], in_[0]), [in_], [out])

    def gather(tag, out, win, lst):
        op("v", tag, lambda: g.vector.tensor_copy(out[0], win[0].indirect(lst[0])), [win, lst], [out])

    def scatter(tag, win, lst, in_):
        op("v", tag, lambda: g.vector.tensor_copy(win[0].indirect(lst[0]), in_[0]), [in_, lst], [win])

    def turns(tag, out, name):
        op("v", tag, lambda: g.vector.transpose(T[out][:, 0:128], T[name][:, 32:160]), [R(name, 32, 160)], [R(out, 0, 128)])
        op("v", tag, lambda: g.vector.transpose(T[out][:, 128:288], T[name][:, 16:176]), [R(name, 16, 176)], [R(out, 128, 288)])

    def turn(tag, out, in_):
        op("v", tag, lambda: g.vector.transpose(out[0], in_[0]), [in_], [out])

    def fill(tag, out, c):
        op("v", tag, lambda: g.vector.memset(out[0], c), [], [out])

    def quant(tag, c, s, in_):
        op("v", tag, lambda: g.vector.quantize_mx(c[0], s[0], in_[0]), [in_], [c, s])

    def act(tag, out, in_, func, bias=0.0, scale=1.0, acc=None, lst=None):
        def fn():
            src = in_[0] if lst is None else in_[0].indirect(lst[0])
            if func is F.Copy:
                return g.scalar.activation(out[0], src, func) if scale == 1.0 else g.scalar.activation(out[0], src, func, scale=scale)
            if acc is None:
                return g.scalar.activation(out[0], src, func, bias=ap(bias), scale=ap(scale))
            return g.scalar.activation(out[0], src, func, bias=ap(bias), scale=ap(scale), accum_out=acc[0])
        op("a", tag, fn, [in_, bias, scale, lst], [out] + ([acc] if acc else []))

    def mx(tag, out, wc_, ws_, xc, xs, extra=()):
        op("p", tag, lambda: g.tensor.matmul_mx(out[0], wc_[0], ws_[0], xc[0], xs[0], True, True), [wc_, ws_, xc, xs], [out], extra=extra)

    def iota(tag, out, pattern, base):
        op("g", tag, lambda: g.iota(out[0], pattern, base, 0, allow_small_or_imprecise_dtypes=True), [], [out])

    def dma(q, tag, out, in_, reads, writes, step=None):
        op(q, tag, lambda: Q[q].dma_start(out, in_), reads, writes, inc=16, step=step)

    def move(step, t, out, in_):
        dma("s", step + str(t), out[0], in_[0], [in_], [out], step)

    def one(name, c):
        return R(name, c, c + 1)

    def lot(name, i, n, m):
        return name + str(m - 1 if i == n - 1 else i * (m - 1) // (n - 1))

    def base(t, r):
        return H * ((t + r + 1) % 2)

    def state(t, a, n):
        return R("xs%d" % t, XB + 4 * a, XB + 4 * (a + n))

    def half(name, t, r):
        return R(name, base(t, r), base(t, r) + H)

    dma("a", "ldu", T.ut[:], T.u[:], [], [R("ut")])
    dma("s", "ldz", T.xz0[:], T.x[:, 4 * H:4 * C], [], [R("xz0")])
    dma("a", "ldx", state(0, 0, H)[0], T.x[:, 0:4 * H], [], [state(0, 0, H)])

    iota("io1", R("c16"), [[16, 16]], 0)
    iota("io2", R("row", 32, 64), [[0, 2], [1, 16]], 0)
    iota("io2", R("row", 64, 96), [[0, 8], [1, 4]], 1)
    iota("io3", R("i16"), [[0, H // 16], [1, 16]], 0)
    iota("io4", R("cnt"), [[4, C]], 0)
    iota("io5", R("row", 0, 16), [[1, 2], [32, 4], [160, 2]], 0)
    iota("io5", R("row", 16, 32), [[1, 2], [32, 4], [-128, 2]], 144)
    iota("io6", R("xi"), [[4 * H, 2], [1 - K, 4], [64, 16]], XB - TOP)
    for pad in (R("ord0", 0, 32), R("fr"), R("top", 0, 32), R("top", 160, 192)):
        fill("z1", pad, 0.0)
    copy("k1", R("ulist"), R("c16", 0, 8))
    ts("k1", R("cn"), R("c16"), 16.0 - TOP, A.add)
    ts("k1", R("sgn1", 15, SLOT[1] * 8, SLOT[1]), R("c16", 0, 8), K + 15.0 - TOP, A.add)
    ts("k1", R("sgn1", SLOT[1] * 8 + 15, None, SLOT[1]), R("c16", 8, 16), 15.0 - TOP, A.add)
    turn("k2", R("col", 32, 96), R("row", 32, 96))
    fill("z2", R("blank", K, 2 * K), 0.0)
    fill("z2", R("ones"), 1.0)
    for r in range(2):
        fill("z3", R("flag%d" % r, 0, None, RUN[r]), -float(MID))
    fill("z3", R("flag0", RUN[0] - 1, None, RUN[0]), 0.0)
    fill("z3", R("ss1", K, K + H + 16), HUGE)
    qcol, tcol = one("col", 32), one("col", 64)
    ts("k3", R("hot"), R("i16"), qcol, A.is_equal)
    act("k9", R("keep0"), R("i16"), F.Sign)
    quant("qu", R("uc"), R("us"), R("ut"))
    ts("kc", one("pc", 0), qcol, float(MARK), A.not_equal)
    act("pv", R("us2"), R("us"), F.Copy, lst=R("ulist"))
    op("v", "pu", lambda: g.vector.tensor_copy(T.uc2[:, 0:128].bitcast(dt.uint32), T.uc[:, 0:128].bitcast(dt.uint32).indirect(T.ulist[:, 0:8])),
       [R("uc"), R("ulist")], [R("uc2")])
    act("kd", one("pc", 1), one("pc", 0), F.Identity, scale=FREE)
    act("kd", one("pc", 2), one("pc", 0), F.Identity, bias=tcol, scale=-1.0)
    act("kd", one("pc", 3), qcol, F.Identity, scale=4.0)
    act("k7", R("src"), R("cnt"), F.Identity, bias=one("pc", 2), scale=one("pc", 0))
    ts("ke", R("keepg"), R("i16"), qcol, A.is_gt)
    turn("k4", R("col", 0, 32), R("row", 0, 32))
    ts("k4", R("rep"), R("c16", 0, 4), 0.0, A.mult, qcol, A.add)
    copy("k6", one("selo", 0), one("col", 0))
    ts("k6", one("selo", 1), one("col", 0), 2.0, A.add)
    ts("k6", one("selv", 0), one("col", 0), float(MARK), A.add)
    act("kf", R("blank", 0, K), R("ones"), F.Identity, scale=one("pc", 1))
    act("kg", R("xo"), R("xi"), F.Identity, bias=one("pc", 3))

    def quantise(t, r):
        quant("q%d" % r, half("qc", t, r), half("qs", t, r), state(t, base(t, 1), H) if r else R("xz%d" % t))

    def scores(bank, t, r):
        mx("m%s%d" % (bank, r), R("p%s%d" % (bank, r), 0, H), R("uc2"), R("us2"), half("qc", t, r), half("qs", t, r))

    def own(tag, a, b):
        tt(tag, R("msk", a, b), R("pd0", a, b), R("hot", 0, b - a), A.mult)

    def keep(tag, a, b):
        scan(tag, R("hold", a, b), R("keep0", 0, b - a), R("msk", a, b), 0.0, A.mult, A.add)

    def count(t, r):
        w = WIDE[r]
        lead = K if r and t % 2 else 0
        s0 = K - lead if r else 0
        if r and not lead:
            sc, vc = range(16 - NS[r], 16), range(16 - NS[r])
            se = sc[NS[r] - NE:]
        else:
            sc, vc = range(NS[r]), range(NS[r], 16)
            se = sc[:NE * r]
        ss, fl, sg, jk, sm = ["%s%d" % (x, r) for x in ("ss", "flag", "sgn", "junk", "sums")]
        vx = (vc[len(vc) - NX:] if lead else vc[:NX]) if r else ()
        first = 1 if lead else 0

        def mine(name, c):
            if r:
                return one(ss, K + 16 * c + 15) if name == "hold" else 0.0
            return one(name, 16 * c + 15)

        def row(a, b, bank):
            if not r:
                return R(bank + "0", a, b)
            return R(ss, s0 + a, s0 + b)

        def sign(tag, c, a, b):
            s = SLOT[r] * c + 16
            act(tag, R(sg, s + a, s + b), row(a, b, "pa"), F.Sign, bias=mine("hold", c), scale=-1.0)

        def add(tag, c, side):
            s, cut = SLOT[r] * c + 16, lead + 16 * c + 16 - r
            if side == 0:
                act(tag, R(jk, s - 1, s + cut), R(sg, s - 1, s + cut), F.Relu, scale=-1.0, acc=one("acc1", 16 * r + c))
            else:
                act(tag, R(jk, s + cut + r, s + w), R(sg, s + cut + r, s + w), F.Relu, acc=one("acc2", 16 * r + c))

        def flags(tag, c, side, only=None):
            f, cut = RUN[r] * c + 1, lead + 16 * c + 16
            a, b, o, d = (0, cut - r, A.is_le, 0) if side == 0 else (cut, w, A.is_lt, r)
            if only is not None:
                edge = lead if lead else H + 16
                a, b = (edge, b) if only == side else (a, edge)
            if a < b:
                ts(tag, R(fl, f + a - d, f + b - d), row(a, b, "pd"), mine("hold", c), o)

        if r:
            act("cp1", R("sr"), R("pa1", 0, H), F.Copy)
            for q in range(16):
                dma("s", "skew%d" % t, T.ss1[q:128:16, K + 15 - q:K + 15 - q + H], T.sr[q:128:16, :], [R("sr")], [R("ss1", K, K + H + 16)], "skew")
        else:
            tt("e0", R("eqs"), R("pd0", 0, H), R("hold"), A.is_equal)
            scan("g0", R("gate"), R("keepg"), R("eqs"), 0.0, A.mult, A.subtract)
            tt("kk0", R(sg, 15, SLOT[0] * NS[0], SLOT[0]), R("gate", 15, 16 * NS[0], 16), R("cn", 0, NS[0]), A.add)
            act("cp0", R(ss), R("pa0", 0, H), F.Copy)
        if r:
            for i, c in enumerate(vc):
                flags("b%d" % (i // 2), c, first)
            for c in vx:
                flags("c0", c, 1 - first, 0)
            for i, c in enumerate(se):
                sign(lot("w", i, len(se), 3), c, lead, lead + H + 16)
            for i, c in enumerate(se):
                add(lot("r", i, len(se), 3), c, first)
            gather("v1", R(ss, 0, K) if lead else R(ss, K + H + 16, 2 * K + H + 16), R("ss0"), R("lst1", 0, 8))
        for i, c in enumerate(vc):
            if not r:
                flags("a0%d" % (i // 2), c, 0)
            flags("a%d%d" % (r, i // 2), c, 1 - first, 1 if c in vx else None)
        for i, c in enumerate(sc):
            sign(lot("x%d" % r, i, len(sc), 3), c, *((0, w) if c not in se else (0, lead) if lead else (H + 16, w)))
        for i, c in enumerate(sc):
            for side in (0, 1):
                if not (c in se and side == first):
                    add(lot("y%d" % r, i, len(sc), 3), c, side)
        m = RUN[r] // 2
        for i, c in enumerate(vc):
            f = RUN[r] * c
            scan(lot("s%d" % r, i, len(vc), 3), R(sm, m * c, m * c + m), R(fl, f, f + m), R(fl, f + m, f + 2 * m), mine("gate", c), A.add, A.add)
        a, b = 16 * r + sc[0], 16 * r + sc[-1] + 1
        tt("t%d" % r, R("s1", a, b), R("acc1", a, b), R("acc2", a, b), A.subtract)
        ends = R(sm, m * vc[0] + m - 1, m * (vc[-1] + 1), m)
        ts("o%d" % r, R("off", 16 * r + vc[0], 16 * r + vc[-1] + 1), ends, float(MID), A.add)
        ts("u%d" % r, R("off", a, b), R("s1", a, b), -1.0, A.mult, float(TOP), A.add)
        if r:
            ts("ov", R("s1", 16 + vc[0], 16 + vc[-1] + 1), ends, -1.0, A.mult, float(TOP - MID), A.add)
        scatter("sc%d" % r, R("ord%d" % r, 32, 32 + H + K * r), R("off", 16 * r, 16 * r + 16), half("src", t, r))

    eng = topo.engines(core, nxt)
    rid, pid = topo.addr(nxt)[0], topo.addr(nxt)[1]
    part = len(eng) // 2
    mask_c = sum(1 << e for e in eng[:part])
    mask_s = sum(1 << e for e in eng[part:part + part // 2])
    arrivals = len(topo.engines(prv, core)) // 2
    arrivals += arrivals // 2

    for t in range(ROUNDS):
        rnd[0] = t
        X, up = "xs%d" % t, t % 2
        quantise(t, 0)
        scores("d", t, 0)
        scores("a", t, 0)
        own("m2", 0, HEAD)
        own("m1", HEAD, H)
        keep("h2", 0, HEAD)
        keep("h1", HEAD, H)
        quantise(t, 1)
        scores("a", t, 1)
        if t == 0:
            dma("s", "lda", T.at[:], T.a[:], [R("xz0"), state(0, 0, H)], [R("at")])
            dma("s", "ldw", T.wcb[:].bitcast(dt.uint8), T.wc[:], [], [R("wcb")], "lda")
            dma("s", "ldw", T.wsb[:], T.ws[:], [], [R("wsb")], "lda")
            dma("s", "ldv", T.vt[:], T.v[:], [], [R("vt")], "lda")
            quant("qa", R("lc0"), R("ls0"), R("at"))
        else:
            p = t - 1
            quant("qp", R("pc%d" % p), R("ps%d" % p), R("pt%d" % p))
            op("g", "sent", lambda p=p: g.remote_dma(T["lc%d" % (p + 1)][:].bitcast(dt.uint8), T["pc%d" % p][:].bitcast(dt.uint8),
                                                     T.sem["arr%d" % (p + 1)], T.sem.sent, pid, rid, mask_c), [R("pc%d" % p)], [], inc=-part)
            op("g", "sent", lambda p=p: g.remote_dma(T["ls%d" % (p + 1)][:], T["ps%d" % p][:],
                                                     T.sem["arr%d" % (p + 1)], T.sem.sent, pid, rid, mask_s), [R("ps%d" % p)], [], inc=-(part // 2))
        if t == 1:
            quant("qv", R("vc"), R("vs"), R("vt"))
        move("free", t, R("ord1", 32, 32 + K), R("blank", K * up, K * up + K))
        move("cpx", t, state(t + 1, base(t, 0), H), R("xz%d" % t))
        if t < ROUNDS - 1:
            move("cpy", t, state(t, base(t, 0), H), R("xz%d" % t))
        count(t, 0)
        turns("tr1", "tt1", "ord0")
        ts("l1", R("lst1"), R("tt1"), 0.25, A.mult, -float(base(t, 0)), A.add, lst=one("selo", 0))
        count(t, 1)
        for b in range(4):
            mx("me", R("pe%d" % b, 0, K), R("wcb", K * b, K * b + K), R("wsb", K * b, K * b + K), R("lc%d" % t), R("ls%d" % t),
               extra=(("arr%d" % t, arrivals),) if t > 0 and b == 0 else ())
        for b in range(4):
            act("relu", R(X, K * b, K * b + K), R("pe%d" % b, 0, K), F.Relu, scale=0.03125)
        ts("ga", R("ga"), R("s1", 16, 32), float(TOP - K), A.is_le, FREE, A.mult)
        tt("gd", R("gd"), R("ga"), R("s1", 16, 32), A.subtract)
        tt("ge", R("ge"), R("gd"), R("xo", 64 * up, 64 * up + 64), A.min, lst=R("rep"))
        ts("gl", R("gl"), R("ge"), float(TOP), A.add)
        end = XB + 4 * (base(t, 1) + H)
        for i in range(NV):
            c = 12 - 4 * i
            gather("gv%d" % i, R("xz%d" % (t + 1), 64 * c + 3, 64 * c + 256, 4), R(X, 3 * K, end), R("gl", 48 + c, 52 + c))
        for e in range(4):
            c = min(16, 64 - 4 * NV - 16 * e)
            act("gz", R("xz%d" % (t + 1), e, 64 * c, 4), R(X, K * e, end), F.Copy, lst=R("gl", 16 * e, 16 * e + c))
        scan("fr", R("fr", 33, 32 + K), R("ones", 0, K - 1), R("ord1", 32, 31 + K), 0.0, A.add, A.subtract)
        turns("trf", "ttf", "fr")
        gather("lf", R("lstf"), R("ttf"), one("selv", 0))
        tt("mg", R("top", 32, 32 + K), R("ord0", 32, 32 + K), R("ord1", 32, 32 + K), A.max if up else A.min, lst=R("lstf", 0, 8))
        turns("tro", "tto", "top")
        gather("lo", R("lst"), R("tto"), R("selo", 0, 2))
        scatter("scy", state(t + 1, 0, C), R("lst", 0, 16), R(X, 0, XB // 2))
        scatter("scx", state(t + 1, 0, C), R("lst", 16, 32), R(X, XB // 2, XB))
        if t < ROUNDS - 1:
            for e in range(4):
                act("gp", R("pt%d" % t, e, 512, 4), state(t, 0, C), F.Copy, lst=R("lst", 8 * e, 8 * e + 8))
        else:
            act("olm", R("olb"), R("top", 32, 32 + K), F.Copy, scale=0.25)
            dma("s", "sto", T.ol[:, :], T.olb[0:128:16, :], [R("olb")], [])

    t = rnd[0] = ROUNDS
    a, b = base(t, 0), base(t, 1)
    quantise(t, 0)
    mx("md0", R("pd0", 0, H), R("vc"), R("vs"), half("qc", t, 0), half("qs", t, 0))
    dma("s", "st0", T.oc[:, 4 * a:4 * (a + H)], half("qc", t, 0)[0].bitcast(dt.uint8), [half("qc", t, 0)], [])
    act("yc0", half("ysb", t, 0), R("pd0", 0, H), F.Copy)
    dma("a", "st1", T.y[:, a:a + H], T.ysb[:, a:a + H], [half("ysb", t, 0)], [])
    quant("q1", R("qc", b, b + K), R("qs", b, b + K), state(t, b, K))
    quant("q2", R("qc", b + K, b + H), R("qs", b + K, b + H), state(t, b + K, K))
    mx("ma1", R("pa1", 0, K), R("vc"), R("vs"), R("qc", b, b + K), R("qs", b, b + K))
    mx("md1", R("pd1", 0, K), R("vc"), R("vs"), R("qc", b + K, b + H), R("qs", b + K, b + H))
    dma("s", "st2", T.oc[:, 4 * b:4 * (b + H)], half("qc", t, 1)[0].bitcast(dt.uint8), [half("qc", t, 1)], [])
    act("yc2", R("ysb", b, b + K), R("pa1", 0, K), F.Copy)
    copy("yc1", R("ysb", b + K, b + H), R("pd1", 0, K))
    dma("a", "st3", T.y[:, b:b + K], T.ysb[:, b:b + K], [R("ysb", b, b + K)], [])
    dma("a", "st5", T.y[:, b + K:b + H], T.ysb[:, b + K:b + H], [R("ysb", b + K, b + H)], [])
    for k in range(4):
        dma("s", "st4", T.osc[4 * k:4 * k + 4, :], T.qs[32 * k:32 * k + 4, :], [R("qs")], [])

    place = {x: i for i, x in enumerate(ORDER.split())}

    def when(o):
        if o["grp"] == ("q1", 0):
            return (-1, place["q0"])
        return (o["grp"][1] - (o["step"] in AHEAD), place[o["step"]])
    ops.sort(key=when)

    total, upto, last = {}, {}, {}
    for i, o in enumerate(ops):
        tag = o["grp"][0]
        total[tag] = total.get(tag, 0) + abs(o["inc"])
        upto[o["grp"]] = total[tag]
        last[o["grp"]] = i
    known = {q: {} for q in Q}
    clock, seen, touched = {}, {}, {}
    for i, o in enumerate(ops):
        q, need = o["q"], []
        for x, writes in [(x, False) for x in o["r"]] + [(x, True) for x in o["w"]]:
            for y, wrote, grp in touched.get(x[0], []):
                if grp != o["grp"] and (writes or wrote) and x[1] & y[1] and grp not in need:
                    need.append(grp)
        need.sort(key=lambda grp: -last[grp])
        for grp in need:
            if known[q].get(grp[0], 0) >= upto[grp]:
                continue
            assert last[grp] < i, (grp, o["grp"])
            Q[q].wait_ge(T.sem[grp[0]], upto[grp])
            seen[grp[0]] = max(seen.get(grp[0], 0), upto[grp])
            for tag, n in clock[grp].items():
                known[q][tag] = max(known[q].get(tag, 0), n)
        for name, n in o["extra"]:
            Q[q].wait_ge(T.sem[name], n)
        ins = o["fn"]()
        if o["inc"] > 0:
            ins.then_inc(T.sem[o["grp"][0]], o["inc"])
        for x in o["r"]:
            touched.setdefault(x[0], []).append((x, False, o["grp"]))
        for x in o["w"]:
            touched.setdefault(x[0], []).append((x, True, o["grp"]))
        if last[o["grp"]] == i:
            clock[o["grp"]] = dict(known[q])
            clock[o["grp"]][o["grp"][0]] = upto[o["grp"]]
    for tag in TAGS:
        if seen.get(tag, 0) < total.get(tag, 0):
            g.wait_ge(T.sem[tag], total[tag])
